import numpy as np
import ml_dtypes


def mxq(x, axis, fmt="e4m3"):
    dtype, down = {"e4m3": (ml_dtypes.float8_e4m3fn, 7), "e5m2": (ml_dtypes.float8_e5m2, 14)}[fmt]
    v = np.moveaxis(np.asarray(x, np.float32).astype(ml_dtypes.bfloat16).astype(np.float64), axis, -1)
    blocks = v.reshape(v.shape[:-1] + (-1, 32))
    amax = np.abs(blocks).max(-1, keepdims=True)
    byte = np.maximum(np.where(amax > 0, np.frexp(amax)[1] - 1 + 127, 0) - down, 1)
    scale = np.exp2(byte - 127.0)
    codes = (blocks / scale).astype(np.float32).astype(dtype).astype(np.float64)
    return np.moveaxis((codes * scale).reshape(v.shape), -1, axis)


WIDE = False


def mx_kscale(k):
    if not WIDE:
        return np.ones(k)
    levels = np.array([10, -10, 5, -5, 0])
    if k % 512:
        return np.exp2(np.random.permutation(np.resize(levels, k // 32))).repeat(32)
    a = np.empty((k // 512, 16))
    for p in range(k // 512):
        a[p, :8] = np.random.permutation(np.resize(levels, 8))
        for g in range(8):
            far = levels[np.abs(levels - a[p, g]) >= 10]
            a[p, g + 8] = far[np.random.randint(len(far))]
    return np.exp2(a.ravel()).repeat(32)


def f64(x):
    return np.asarray(x).astype(np.float64)


def striped(idx):
    return np.tile(idx.reshape(-1, 16).T, (8, 1)).astype(np.uint16)


def unstriped(offs):
    return offs[:16].T.reshape(-1).astype(np.int64)


def pack_weight(w):
    k, n = w.shape
    w = f64(np.asarray(w, np.float32).astype(ml_dtypes.bfloat16)).reshape(k // 32, 32, n)
    amax = np.abs(w).max(1)
    byte = np.clip(np.where(amax > 0, np.frexp(amax)[1] - 1 + 127 - 7, 1), 1, 254)
    scaled = (w * np.exp2(127.0 - byte)[:, None, :]).reshape(k, n).astype(np.float32)
    words = np.ascontiguousarray(scaled.reshape(k // 512, 128, 4, n).transpose(0, 1, 3, 2)).astype(ml_dtypes.float8_e4m3fn).view(np.uint8)
    return words, np.ascontiguousarray(byte.astype(np.uint8).reshape(k // 512, 16, n))


def unpack_weight(words, scales):
    g, p, n, _ = words.shape
    vals = np.ascontiguousarray(words).view(ml_dtypes.float8_e4m3fn).astype(np.float64) * np.repeat(np.exp2(scales.astype(np.float64) - 127.0), 8, axis=1)[..., None]
    return vals.transpose(0, 1, 3, 2).reshape(g * 512, n)


def sigmoid(v):
    return 1.0 / (1.0 + np.exp(-np.maximum(v, -700.0)))


K, T, S, V, N = 512, 4096, 1024, 512, 128


def setup_inputs():
    n = np.random.standard_normal
    s = mx_kscale(K)[:, None]
    packed_w1 = pack_weight(n((K, N)) / np.sqrt(K) / s)
    return {
        "xT": (n((K, T)) * s).astype(np.float32),
        "w1_words": packed_w1[0],
        "w1_scales": packed_w1[1],
        "offs": striped(np.random.permutation(T)[:S]),
        "win": striped(np.random.permutation(S)[:V]),
        "lose": striped(np.random.permutation(S)[:V]),
    }


def reference(xT, w1_words, w1_scales, offs, win, lose):
    xq = mxq(f64(xT)[:, unstriped(offs)], 0, "e4m3")
    y = unpack_weight(w1_words, w1_scales).T @ xq
    return sigmoid(y[:, unstriped(win)] - y[:, unstriped(lose)])

@@ -1,0 +1,131 @@
+from contextlib import ExitStack
+
+import concourse.mybir as mybir
+
+K, T, S, V, N = 512, 4096, 1024, 512, 128
+FLOPS = 2 * K * S * N
+
+F32 = mybir.dt.float32
+BF16 = mybir.dt.bfloat16
+I32 = mybir.dt.int32
+U32 = mybir.dt.uint32
+U16 = mybir.dt.uint16
+U8 = mybir.dt.uint8
+FP8X4 = mybir.dt.float8_e4m3fn_x4
+ACT = mybir.ActivationFunctionType
+ALU = mybir.AluOpType
+
+P = 128
+PACK = 4
+HALF = S // 2
+LIST_ROWS = 16
+BANK = 512
+LAST_CHUNKS = (1024, 1024, 896, 896, 256)
+SCALAR_CHUNKS = 3
+HEAD_PIECES = (128, 128, 256)
+TAIL_PIECES = (256, 128, 128)
+PAIR_PIECES = (256, 128, 128)
+
+
+def spans(widths):
+    starts = [sum(widths[:i]) for i in range(len(widths))]
+    return [slice(a, a + w) for a, w in zip(starts, widths)]
+
+
+def list_cols(entries):
+    return slice(entries.start // LIST_ROWS, entries.stop // LIST_ROWS)
+
+
+def tile_picked_ranknet_sigmoid_e_kernel(tc, xT, w1_words, w1_scales, offs, win, lose, out):
+    nc = tc.nc
+    with ExitStack() as ctx:
+        keep = ctx.enter_context(tc.tile_pool(name="keep", bufs=1))
+        psum = ctx.enter_context(tc.psum_pool(name="psum", bufs=1))
+
+        offs_sb = keep.tile([P, S // LIST_ROWS], U16, name="offs_sb")
+        win_sb = keep.tile([P, V // LIST_ROWS], U16, name="win_sb")
+        lose_sb = keep.tile([P, V // LIST_ROWS], U16, name="lose_sb")
+        w_codes = keep.tile([P, N], U32, name="w_codes", align_bytes=64)
+        w_scale = keep.tile([P, N], U8, name="w_scale", align_bytes=64)
+        rows = [keep.tile([P, T], F32, name="rows%d" % j) for j in range(PACK)]
+        rows_bf = {j: keep.tile([P, T], BF16, name="rows_bf%d" % j) for j in (2, 3)}
+        x_rows = xT.rearrange("(p j) t -> p j t", j=PACK)
+
+        nc.sync.dma_start(out=rows[2][:], in_=x_rows[:, 2, :])
+        nc.sync.dma_start(offs_sb[:], offs)
+        nc.sync.dma_start(out=rows[0][:], in_=x_rows[:, 0, :])
+        nc.sync.dma_start(out=rows[1][:], in_=x_rows[:, 1, :])
+        for cols in spans(LAST_CHUNKS):
+            nc.sync.dma_start(out=rows[3][:, cols], in_=x_rows[:, 3, cols])
+        nc.sync.dma_start(out=w_codes[:].bitcast(I32), in_=w1_words[0].rearrange("p n t -> p (n t)").bitcast(I32))
+        nc.sync.dma_start(win_sb[:], win)
+        nc.sync.dma_start(lose_sb[:], lose)
+
+        nc.gpsimd.memset(w_scale[:], 0)
+        for q in range(4):
+            nc.gpsimd.dma_start(
+                out=w_scale[:].bitcast(I32)[32 * q : 32 * q + 4, :],
+                in_=w1_scales[0, 4 * q : 4 * q + 4, :].bitcast(I32),
+            )
+
+        picked = [keep.tile([P, HALF, PACK], BF16, name="picked%d" % h, align_bytes=64) for h in range(2)]
+        y = keep.tile([P, S], F32, name="y")
+        halves = [offs_sb[:, list_cols(slice(h * HALF, (h + 1) * HALF))] for h in range(2)]
+
+        nc.vector.tensor_copy(picked[0][:, :, 2], rows[2][:].indirect(halves[0]))
+        nc.scalar.activation(rows_bf[2][:], rows[2][:], ACT.Copy)
+        nc.scalar.activation(picked[1][:, :, 2], rows_bf[2][:].indirect(halves[1]), ACT.Copy)
+        for j in (0, 1):
+            for h in range(2):
+                nc.vector.tensor_copy(picked[h][:, :, j], rows[j][:].indirect(halves[h]))
+        for i, cols in enumerate(spans(LAST_CHUNKS)):
+            if i < SCALAR_CHUNKS:
+                nc.scalar.activation(rows_bf[3][:, cols], rows[3][:, cols], ACT.Copy)
+            else:
+                nc.vector.tensor_copy(rows_bf[3][:, cols], rows[3][:, cols])
+        nc.scalar.activation(picked[1][:, :, 3], rows_bf[3][:].indirect(halves[1]), ACT.Copy)
+        nc.vector.tensor_copy(picked[0][:, :, 3], rows[3][:].indirect(halves[0]))
+
+        def score(h, cols, acc):
+            width = cols.stop - cols.start
+            codes = keep.tile([P, width], U32, name="codes%d_%d" % (h, cols.start), align_bytes=64)
+            scales = keep.tile([P, width], U8, name="scales%d_%d" % (h, cols.start), align_bytes=64)
+            nc.vector.quantize_mx(
+                out=codes[:].bitcast(FP8X4),
+                scales=scales[:],
+                in_=picked[h][:, cols, :].rearrange("p n j -> p (n j)"),
+            )
+            nc.tensor.matmul_mx(
+                out=acc,
+                lhsT=w_codes[:].bitcast(FP8X4),
+                lhsT_scale=w_scale[:],
+                rhs=codes[:].bitcast(FP8X4),
+                rhs_scale=scales[:],
+                start=True,
+                stop=True,
+            )
+
+        first_bank = psum.tile([P, BANK], F32, name="first_bank")
+        for cols in spans(HEAD_PIECES):
+            score(0, cols, first_bank[:, cols])
+        tail_banks = [psum.tile([P, BANK], F32, name="tail_bank%d" % i) for i in range(len(TAIL_PIECES))]
+        for bank, cols in zip(tail_banks, spans(TAIL_PIECES)):
+            score(1, cols, bank[:, : cols.stop - cols.start])
+        nc.scalar.activation(y[:, :HALF], first_bank[:], ACT.Copy)
+        for i, (bank, cols) in enumerate(zip(tail_banks, spans(TAIL_PIECES))):
+            y_cols = y[:, HALF + cols.start : HALF + cols.stop]
+            if i == 0:
+                nc.scalar.activation(y_cols, bank[:, : cols.stop - cols.start], ACT.Copy)
+            else:
+                nc.vector.tensor_copy(y_cols, bank[:, : cols.stop - cols.start])
+
+        y_win = keep.tile([P, V], F32, name="y_win")
+        for cols in spans((V // 2, V // 2)):
+            nc.vector.tensor_copy(y_win[:, cols], y[:].indirect(win_sb[:, list_cols(cols)]))
+        for cols in spans(PAIR_PIECES):
+            width = cols.stop - cols.start
+            gap = keep.tile([P, width], F32, name="gap%d" % cols.start)
+            prob = keep.tile([P, width], F32, name="prob%d" % cols.start)
+            nc.vector.tensor_tensor(gap[:], y[:].indirect(lose_sb[:, list_cols(cols)]), y_win[:, cols], ALU.subtract)
+            nc.scalar.activation(prob[:], gap[:], ACT.Sigmoid, scale=-1.0)
+            nc.sync.dma_start(out=out[:, cols], in_=prob[:])

@@ -20,11 +20,11 @@ PACK = 4
 HALF = S // 2
 LIST_ROWS = 16
 BANK = 512
-LAST_CHUNKS = (1024, 1024, 896, 896, 256)
-SCALAR_CHUNKS = 3
-HEAD_PIECES = (128, 128, 256)
-TAIL_PIECES = (256, 128, 128)
-PAIR_PIECES = (256, 128, 128)
+LAST_CHUNKS = (1024, 1024, 1024, 512, 512)
+VECTOR_CHUNK = 3
+SCORE_PIECES = (256, 256, 128, 128, 128, 128)
+VECTOR_BANKS = (2, 3)
+PAIR_PIECES = (256, 192, 64)
 
 
 def spans(widths):
@@ -61,9 +61,9 @@ def tile_picked_ranknet_sigmoid_e_kernel(tc, xT, w1_words, w1_scales, offs, win,
         nc.sync.dma_start(win_sb[:], win)
         nc.sync.dma_start(lose_sb[:], lose)
 
-        nc.gpsimd.memset(w_scale[:], 0)
+        nc.vector.memset(w_scale[:].bitcast(I32), 0)
         for q in range(4):
-            nc.gpsimd.dma_start(
+            nc.scalar.dma_start(
                 out=w_scale[:].bitcast(I32)[32 * q : 32 * q + 4, :],
                 in_=w1_scales[0, 4 * q : 4 * q + 4, :].bitcast(I32),
             )
@@ -79,24 +79,27 @@ def tile_picked_ranknet_sigmoid_e_kernel(tc, xT, w1_words, w1_scales, offs, win,
             for h in range(2):
                 nc.vector.tensor_copy(picked[h][:, :, j], rows[j][:].indirect(halves[h]))
         for i, cols in enumerate(spans(LAST_CHUNKS)):
-            if i < SCALAR_CHUNKS:
-                nc.scalar.activation(rows_bf[3][:, cols], rows[3][:, cols], ACT.Copy)
-            else:
+            if i == VECTOR_CHUNK:
                 nc.vector.tensor_copy(rows_bf[3][:, cols], rows[3][:, cols])
+            else:
+                nc.scalar.activation(rows_bf[3][:, cols], rows[3][:, cols], ACT.Copy)
         nc.scalar.activation(picked[1][:, :, 3], rows_bf[3][:].indirect(halves[1]), ACT.Copy)
         nc.vector.tensor_copy(picked[0][:, :, 3], rows[3][:].indirect(halves[0]))
 
-        def score(h, cols, acc):
+        banks = []
+        for i, cols in enumerate(spans(SCORE_PIECES)):
             width = cols.stop - cols.start
-            codes = keep.tile([P, width], U32, name="codes%d_%d" % (h, cols.start), align_bytes=64)
-            scales = keep.tile([P, width], U8, name="scales%d_%d" % (h, cols.start), align_bytes=64)
+            h, first = divmod(cols.start, HALF)
+            codes = keep.tile([P, width], U32, name="codes%d" % i, align_bytes=64)
+            scales = keep.tile([P, width], U8, name="scales%d" % i, align_bytes=64)
             nc.vector.quantize_mx(
                 out=codes[:].bitcast(FP8X4),
                 scales=scales[:],
-                in_=picked[h][:, cols, :].rearrange("p n j -> p (n j)"),
+                in_=picked[h][:, first : first + width, :].rearrange("p n j -> p (n j)"),
             )
+            bank = psum.tile([P, BANK], F32, name="bank%d" % i)
             nc.tensor.matmul_mx(
-                out=acc,
+                out=bank[:, :width],
                 lhsT=w_codes[:].bitcast(FP8X4),
                 lhsT_scale=w_scale[:],
                 rhs=codes[:].bitcast(FP8X4),
@@ -104,20 +107,12 @@ def tile_picked_ranknet_sigmoid_e_kernel(tc, xT, w1_words, w1_scales, offs, win,
                 start=True,
                 stop=True,
             )
-
-        first_bank = psum.tile([P, BANK], F32, name="first_bank")
-        for cols in spans(HEAD_PIECES):
-            score(0, cols, first_bank[:, cols])
-        tail_banks = [psum.tile([P, BANK], F32, name="tail_bank%d" % i) for i in range(len(TAIL_PIECES))]
-        for bank, cols in zip(tail_banks, spans(TAIL_PIECES)):
-            score(1, cols, bank[:, : cols.stop - cols.start])
-        nc.scalar.activation(y[:, :HALF], first_bank[:], ACT.Copy)
-        for i, (bank, cols) in enumerate(zip(tail_banks, spans(TAIL_PIECES))):
-            y_cols = y[:, HALF + cols.start : HALF + cols.stop]
-            if i == 0:
-                nc.scalar.activation(y_cols, bank[:, : cols.stop - cols.start], ACT.Copy)
+            banks.append(bank[:, :width])
+        for i, cols in enumerate(spans(SCORE_PIECES)):
+            if i in VECTOR_BANKS:
+                nc.vector.tensor_copy(y[:, cols], banks[i])
             else:
-                nc.vector.tensor_copy(y_cols, bank[:, : cols.stop - cols.start])
+                nc.scalar.activation(y[:, cols], banks[i], ACT.Copy)
 
         y_win = keep.tile([P, V], F32, name="y_win")
         for cols in spans((V // 2, V // 2)):

@@ -20,10 +20,10 @@ PACK = 4
 HALF = S // 2
 LIST_ROWS = 16
 BANK = 512
-LAST_CHUNKS = (1024, 1024, 1024, 512, 512)
-VECTOR_CHUNK = 3
-SCORE_PIECES = (256, 256, 128, 128, 128, 128)
-VECTOR_BANKS = (2, 3)
+LAST_CHUNKS = (1024, 1024, 1024, 512, 256, 256)
+VECTOR_CHUNKS = (3, 4)
+SCORE_PIECES = (256, 256, 128, 128, 128, 64, 64)
+VECTOR_BANKS = (3, 5)
 PAIR_PIECES = (256, 192, 64)
 
 
@@ -79,7 +79,7 @@ def tile_picked_ranknet_sigmoid_e_kernel(tc, xT, w1_words, w1_scales, offs, win,
             for h in range(2):
                 nc.vector.tensor_copy(picked[h][:, :, j], rows[j][:].indirect(halves[h]))
         for i, cols in enumerate(spans(LAST_CHUNKS)):
-            if i == VECTOR_CHUNK:
+            if i in VECTOR_CHUNKS:
                 nc.vector.tensor_copy(rows_bf[3][:, cols], rows[3][:, cols])
             else:
                 nc.scalar.activation(rows_bf[3][:, cols], rows[3][:, cols], ACT.Copy)

@@ -58,15 +58,14 @@ def tile_picked_ranknet_sigmoid_e_kernel(tc, xT, w1_words, w1_scales, offs, win,
         for cols in spans(LAST_CHUNKS):
             nc.sync.dma_start(out=rows[3][:, cols], in_=x_rows[:, 3, cols])
         nc.sync.dma_start(out=w_codes[:].bitcast(I32), in_=w1_words[0].rearrange("p n t -> p (n t)").bitcast(I32))
-        nc.sync.dma_start(win_sb[:], win)
-        nc.sync.dma_start(lose_sb[:], lose)
-
         nc.vector.memset(w_scale[:].bitcast(I32), 0)
         for q in range(4):
-            nc.scalar.dma_start(
+            nc.sync.dma_start(
                 out=w_scale[:].bitcast(I32)[32 * q : 32 * q + 4, :],
                 in_=w1_scales[0, 4 * q : 4 * q + 4, :].bitcast(I32),
             )
+        nc.sync.dma_start(win_sb[:], win)
+        nc.sync.dma_start(lose_sb[:], lose)
 
         picked = [keep.tile([P, HALF, PACK], BF16, name="picked%d" % h, align_bytes=64) for h in range(2)]
         y = keep.tile([P, S], F32, name="y")

@@ -20,11 +20,12 @@ PACK = 4
 HALF = S // 2
 LIST_ROWS = 16
 BANK = 512
-LAST_CHUNKS = (1024, 1024, 1024, 512, 256, 256)
-VECTOR_CHUNKS = (3, 4)
+LAST_CHUNKS = (1536, 1344, 960, 256)
+VECTOR_ROUNDS = (0, 512, 704, 0)
 SCORE_PIECES = (256, 256, 128, 128, 128, 64, 64)
-VECTOR_BANKS = (3, 5)
-PAIR_PIECES = (256, 192, 64)
+VECTOR_BANKS = (3, 5,)
+WIN_PIECES = (256, 256)
+PAIR_PIECES = (192, 160, 160)
 
 
 def spans(widths):
@@ -77,11 +78,12 @@ def tile_picked_ranknet_sigmoid_e_kernel(tc, xT, w1_words, w1_scales, offs, win,
         for j in (0, 1):
             for h in range(2):
                 nc.vector.tensor_copy(picked[h][:, :, j], rows[j][:].indirect(halves[h]))
-        for i, cols in enumerate(spans(LAST_CHUNKS)):
-            if i in VECTOR_CHUNKS:
-                nc.vector.tensor_copy(rows_bf[3][:, cols], rows[3][:, cols])
-            else:
-                nc.scalar.activation(rows_bf[3][:, cols], rows[3][:, cols], ACT.Copy)
+        for cols, by_vector in zip(spans(LAST_CHUNKS), VECTOR_ROUNDS):
+            split = cols.stop - by_vector
+            if split > cols.start:
+                nc.scalar.activation(rows_bf[3][:, cols.start : split], rows[3][:, cols.start : split], ACT.Copy)
+            if by_vector > 0:
+                nc.vector.tensor_copy(rows_bf[3][:, split : cols.stop], rows[3][:, split : cols.stop])
         nc.scalar.activation(picked[1][:, :, 3], rows_bf[3][:].indirect(halves[1]), ACT.Copy)
         nc.vector.tensor_copy(picked[0][:, :, 3], rows[3][:].indirect(halves[0]))
 
@@ -114,7 +116,7 @@ def tile_picked_ranknet_sigmoid_e_kernel(tc, xT, w1_words, w1_scales, offs, win,
                 nc.scalar.activation(y[:, cols], banks[i], ACT.Copy)
 
         y_win = keep.tile([P, V], F32, name="y_win")
-        for cols in spans((V // 2, V // 2)):
+        for cols in spans(WIN_PIECES):
             nc.vector.tensor_copy(y_win[:, cols], y[:].indirect(win_sb[:, list_cols(cols)]))
         for cols in spans(PAIR_PIECES):
             width = cols.stop - cols.start

@@ -20,10 +20,10 @@ PACK = 4
 HALF = S // 2
 LIST_ROWS = 16
 BANK = 512
-LAST_CHUNKS = (1536, 1344, 960, 256)
-VECTOR_ROUNDS = (0, 512, 704, 0)
-SCORE_PIECES = (256, 256, 128, 128, 128, 64, 64)
-VECTOR_BANKS = (3, 5,)
+LAST_CHUNKS = (1856, 1600, 512, 128)
+VECTOR_ROUNDS = (768, 1056, 336, 0)
+SCORE_PIECES = (256, 256, 256, 128, 128)
+VECTOR_BANKS = (2, 4,)
 WIN_PIECES = (256, 256)
 PAIR_PIECES = (192, 160, 160)
 

@@ -22,8 +22,8 @@ LIST_ROWS = 16
 BANK = 512
 LAST_CHUNKS = (1856, 1600, 512, 128)
 VECTOR_ROUNDS = (768, 1056, 336, 0)
-SCORE_PIECES = (256, 256, 256, 128, 128)
-VECTOR_BANKS = (2, 4,)
+SCORE_PIECES = (256, 256, 128, 128, 128, 64, 64)
+VECTOR_BANKS = (3, 5,)
 WIN_PIECES = (256, 256)
 PAIR_PIECES = (192, 160, 160)
 

@@ -20,8 +20,8 @@ PACK = 4
 HALF = S // 2
 LIST_ROWS = 16
 BANK = 512
-LAST_CHUNKS = (1856, 1600, 512, 128)
-VECTOR_ROUNDS = (768, 1056, 336, 0)
+LAST_CHUNKS = (2080, 1376, 480, 160)
+VECTOR_ROUNDS = (800, 864, 288, 0)
 SCORE_PIECES = (256, 256, 128, 128, 128, 64, 64)
 VECTOR_BANKS = (3, 5,)
 WIN_PIECES = (256, 256)

@@ -20,16 +20,17 @@ PACK = 4
 HALF = S // 2
 LIST_ROWS = 16
 BANK = 512
-LAST_CHUNKS = (2080, 1376, 480, 160)
-VECTOR_ROUNDS = (800, 864, 288, 0)
+LAST_CHUNKS = (2816, 960, 320)
+VECTOR_ROUNDS = (1856, 672, 0)
+DENSE_PIECES = (256, 256)
 SCORE_PIECES = (256, 256, 128, 128, 128, 64, 64)
-VECTOR_BANKS = (3, 5,)
+VECTOR_BANKS = (3, 5)
 WIN_PIECES = (256, 256)
 PAIR_PIECES = (192, 160, 160)
 
 
-def spans(widths):
-    starts = [sum(widths[:i]) for i in range(len(widths))]
+def spans(widths, first=0):
+    starts = [first + sum(widths[:i]) for i in range(len(widths))]
     return [slice(a, a + w) for a, w in zip(starts, widths)]
 
 
@@ -49,13 +50,13 @@ def tile_picked_ranknet_sigmoid_e_kernel(tc, xT, w1_words, w1_scales, offs, win,
         w_codes = keep.tile([P, N], U32, name="w_codes", align_bytes=64)
         w_scale = keep.tile([P, N], U8, name="w_scale", align_bytes=64)
         rows = [keep.tile([P, T], F32, name="rows%d" % j) for j in range(PACK)]
-        rows_bf = {j: keep.tile([P, T], BF16, name="rows_bf%d" % j) for j in (2, 3)}
+        last_bf = keep.tile([P, T], BF16, name="last_bf")
         x_rows = xT.rearrange("(p j) t -> p j t", j=PACK)
 
-        nc.sync.dma_start(out=rows[2][:], in_=x_rows[:, 2, :])
-        nc.sync.dma_start(offs_sb[:], offs)
         nc.sync.dma_start(out=rows[0][:], in_=x_rows[:, 0, :])
+        nc.sync.dma_start(offs_sb[:], offs)
         nc.sync.dma_start(out=rows[1][:], in_=x_rows[:, 1, :])
+        nc.sync.dma_start(out=rows[2][:], in_=x_rows[:, 2, :])
         for cols in spans(LAST_CHUNKS):
             nc.sync.dma_start(out=rows[3][:, cols], in_=x_rows[:, 3, cols])
         nc.sync.dma_start(out=w_codes[:].bitcast(I32), in_=w1_words[0].rearrange("p n t -> p (n t)").bitcast(I32))
@@ -72,19 +73,22 @@ def tile_picked_ranknet_sigmoid_e_kernel(tc, xT, w1_words, w1_scales, offs, win,
         y = keep.tile([P, S], F32, name="y")
         halves = [offs_sb[:, list_cols(slice(h * HALF, (h + 1) * HALF))] for h in range(2)]
 
-        nc.vector.tensor_copy(picked[0][:, :, 2], rows[2][:].indirect(halves[0]))
-        nc.scalar.activation(rows_bf[2][:], rows[2][:], ACT.Copy)
-        nc.scalar.activation(picked[1][:, :, 2], rows_bf[2][:].indirect(halves[1]), ACT.Copy)
         for j in (0, 1):
             for h in range(2):
                 nc.vector.tensor_copy(picked[h][:, :, j], rows[j][:].indirect(halves[h]))
+        for cols in spans(DENSE_PIECES):
+            dense = keep.tile([P, cols.stop - cols.start], BF16, name="dense%d" % cols.start)
+            entries = slice(HALF + cols.start, HALF + cols.stop)
+            nc.vector.tensor_copy(dense[:], rows[2][:].indirect(offs_sb[:, list_cols(entries)]))
+            nc.scalar.activation(picked[1][:, cols, 2], dense[:], ACT.Copy)
+        nc.vector.tensor_copy(picked[0][:, :, 2], rows[2][:].indirect(halves[0]))
         for cols, by_vector in zip(spans(LAST_CHUNKS), VECTOR_ROUNDS):
             split = cols.stop - by_vector
             if split > cols.start:
-                nc.scalar.activation(rows_bf[3][:, cols.start : split], rows[3][:, cols.start : split], ACT.Copy)
+                nc.scalar.activation(last_bf[:, cols.start : split], rows[3][:, cols.start : split], ACT.Copy)
             if by_vector > 0:
-                nc.vector.tensor_copy(rows_bf[3][:, split : cols.stop], rows[3][:, split : cols.stop])
-        nc.scalar.activation(picked[1][:, :, 3], rows_bf[3][:].indirect(halves[1]), ACT.Copy)
+                nc.vector.tensor_copy(last_bf[:, split : cols.stop], rows[3][:, split : cols.stop])
+        nc.scalar.activation(picked[1][:, :, 3], last_bf[:].indirect(halves[1]), ACT.Copy)
         nc.vector.tensor_copy(picked[0][:, :, 3], rows[3][:].indirect(halves[0]))
 
         banks = []

@@ -22,7 +22,6 @@ LIST_ROWS = 16
 BANK = 512
 LAST_CHUNKS = (2816, 960, 320)
 VECTOR_ROUNDS = (1856, 672, 0)
-DENSE_PIECES = (256, 256)
 SCORE_PIECES = (256, 256, 128, 128, 128, 64, 64)
 VECTOR_BANKS = (3, 5)
 WIN_PIECES = (256, 256)
@@ -49,13 +48,13 @@ def tile_picked_ranknet_sigmoid_e_kernel(tc, xT, w1_words, w1_scales, offs, win,
         lose_sb = keep.tile([P, V // LIST_ROWS], U16, name="lose_sb")
         w_codes = keep.tile([P, N], U32, name="w_codes", align_bytes=64)
         w_scale = keep.tile([P, N], U8, name="w_scale", align_bytes=64)
-        rows = [keep.tile([P, T], F32, name="rows%d" % j) for j in range(PACK)]
+        rows01 = keep.tile([P, 2, T], F32, name="rows01")
+        rows = {j: keep.tile([P, T], F32, name="rows%d" % j) for j in (2, 3)}
         last_bf = keep.tile([P, T], BF16, name="last_bf")
         x_rows = xT.rearrange("(p j) t -> p j t", j=PACK)
 
-        nc.sync.dma_start(out=rows[0][:], in_=x_rows[:, 0, :])
+        nc.sync.dma_start(out=rows01[:], in_=x_rows[:, 0:2, :])
         nc.sync.dma_start(offs_sb[:], offs)
-        nc.sync.dma_start(out=rows[1][:], in_=x_rows[:, 1, :])
         nc.sync.dma_start(out=rows[2][:], in_=x_rows[:, 2, :])
         for cols in spans(LAST_CHUNKS):
             nc.sync.dma_start(out=rows[3][:, cols], in_=x_rows[:, 3, cols])
@@ -73,14 +72,17 @@ def tile_picked_ranknet_sigmoid_e_kernel(tc, xT, w1_words, w1_scales, offs, win,
         y = keep.tile([P, S], F32, name="y")
         halves = [offs_sb[:, list_cols(slice(h * HALF, (h + 1) * HALF))] for h in range(2)]
 
+        pairs0 = keep.tile([P, HALF, 2], BF16, name="pairs0")
+        pairs1 = keep.tile([P, 2, HALF, 2], BF16, name="pairs1")
+        nc.vector.memset(pairs1[:, 1].rearrange("p n e -> p (n e)").bitcast(I32), 0)
+        words = [picked[h][:].rearrange("p n j -> p (n j)").bitcast(U32).rearrange("p (n u) -> p n u", u=2) for h in range(2)]
         for j in (0, 1):
-            for h in range(2):
-                nc.vector.tensor_copy(picked[h][:, :, j], rows[j][:].indirect(halves[h]))
-        for cols in spans(DENSE_PIECES):
-            dense = keep.tile([P, cols.stop - cols.start], BF16, name="dense%d" % cols.start)
-            entries = slice(HALF + cols.start, HALF + cols.stop)
-            nc.vector.tensor_copy(dense[:], rows[2][:].indirect(offs_sb[:, list_cols(entries)]))
-            nc.scalar.activation(picked[1][:, cols, 2], dense[:], ACT.Copy)
+            nc.vector.tensor_copy(pairs0[:, :, j], rows01[:, j, :].indirect(halves[0]))
+        nc.scalar.copy(words[0], pairs0[:].rearrange("p n e -> p (n e)").bitcast(U32).unsqueeze(2).to_broadcast([P, HALF, 2]))
+        for j in (0, 1):
+            nc.vector.tensor_copy(pairs1[:, 0, :, j], rows01[:, j, :].indirect(halves[1]))
+        nc.vector.tensor_copy(pairs1[:, 1, :, 0], rows[2][:].indirect(halves[1]))
+        nc.scalar.copy(words[1], pairs1[:].rearrange("p u n e -> p u (n e)").bitcast(U32).rearrange("p u n -> p n u"))
         nc.vector.tensor_copy(picked[0][:, :, 2], rows[2][:].indirect(halves[0]))
         for cols, by_vector in zip(spans(LAST_CHUNKS), VECTOR_ROUNDS):
             split = cols.stop - by_vector

@@ -25,7 +25,7 @@ VECTOR_ROUNDS = (1856, 672, 0)
 SCORE_PIECES = (256, 256, 128, 128, 128, 64, 64)
 VECTOR_BANKS = (3, 5)
 WIN_PIECES = (256, 256)
-PAIR_PIECES = (192, 160, 160)
+PAIR_PIECES = (160, 160, 192)
 
 
 def spans(widths, first=0):

@@ -72,17 +72,16 @@ def tile_picked_ranknet_sigmoid_e_kernel(tc, xT, w1_words, w1_scales, offs, win,
         y = keep.tile([P, S], F32, name="y")
         halves = [offs_sb[:, list_cols(slice(h * HALF, (h + 1) * HALF))] for h in range(2)]
 
-        pairs0 = keep.tile([P, HALF, 2], BF16, name="pairs0")
-        pairs1 = keep.tile([P, 2, HALF, 2], BF16, name="pairs1")
-        nc.vector.memset(pairs1[:, 1].rearrange("p n e -> p (n e)").bitcast(I32), 0)
+        pairs = keep.tile([P, 2, HALF, 2], BF16, name="pairs")
+        pair_words = pairs[:].rearrange("p u n e -> p u (n e)").bitcast(U32)
         words = [picked[h][:].rearrange("p n j -> p (n j)").bitcast(U32).rearrange("p (n u) -> p n u", u=2) for h in range(2)]
         for j in (0, 1):
-            nc.vector.tensor_copy(pairs0[:, :, j], rows01[:, j, :].indirect(halves[0]))
-        nc.scalar.copy(words[0], pairs0[:].rearrange("p n e -> p (n e)").bitcast(U32).unsqueeze(2).to_broadcast([P, HALF, 2]))
+            nc.vector.tensor_copy(pairs[:, 1, :, j], rows01[:, j, :].indirect(halves[0]))
+        nc.scalar.copy(words[0], pair_words[:, 1, :].unsqueeze(2).to_broadcast([P, HALF, 2]))
         for j in (0, 1):
-            nc.vector.tensor_copy(pairs1[:, 0, :, j], rows01[:, j, :].indirect(halves[1]))
-        nc.vector.tensor_copy(pairs1[:, 1, :, 0], rows[2][:].indirect(halves[1]))
-        nc.scalar.copy(words[1], pairs1[:].rearrange("p u n e -> p u (n e)").bitcast(U32).rearrange("p u n -> p n u"))
+            nc.vector.tensor_copy(pairs[:, 0, :, j], rows01[:, j, :].indirect(halves[1]))
+        nc.vector.tensor_copy(pairs[:, 1, :, 0], rows[2][:].indirect(halves[1]))
+        nc.scalar.copy(words[1], pair_words.rearrange("p u n -> p n u"))
         nc.vector.tensor_copy(picked[0][:, :, 2], rows[2][:].indirect(halves[0]))
         for cols, by_vector in zip(spans(LAST_CHUNKS), VECTOR_ROUNDS):
             split = cols.stop - by_vector

@@ -25,7 +25,7 @@ VECTOR_ROUNDS = (1856, 672, 0)
 SCORE_PIECES = (256, 256, 128, 128, 128, 64, 64)
 VECTOR_BANKS = (3, 5)
 WIN_PIECES = (256, 256)
-PAIR_PIECES = (160, 160, 192)
+STORES = ((160,), (160,), (128, 64))
 
 
 def spans(widths, first=0):
@@ -123,10 +123,10 @@ def tile_picked_ranknet_sigmoid_e_kernel(tc, xT, w1_words, w1_scales, offs, win,
         y_win = keep.tile([P, V], F32, name="y_win")
         for cols in spans(WIN_PIECES):
             nc.vector.tensor_copy(y_win[:, cols], y[:].indirect(win_sb[:, list_cols(cols)]))
-        for cols in spans(PAIR_PIECES):
-            width = cols.stop - cols.start
-            gap = keep.tile([P, width], F32, name="gap%d" % cols.start)
-            prob = keep.tile([P, width], F32, name="prob%d" % cols.start)
-            nc.vector.tensor_tensor(gap[:], y[:].indirect(lose_sb[:, list_cols(cols)]), y_win[:, cols], ALU.subtract)
-            nc.scalar.activation(prob[:], gap[:], ACT.Sigmoid, scale=-1.0)
-            nc.sync.dma_start(out=out[:, cols], in_=prob[:])
+        for stored, widths in zip(spans([sum(widths) for widths in STORES]), STORES):
+            prob = keep.tile([P, sum(widths)], F32, name="prob%d" % stored.start)
+            for cols, within in zip(spans(widths, stored.start), spans(widths)):
+                gap = keep.tile([P, cols.stop - cols.start], F32, name="gap%d" % cols.start)
+                nc.vector.tensor_tensor(gap[:], y[:].indirect(lose_sb[:, list_cols(cols)]), y_win[:, cols], ALU.subtract)
+                nc.scalar.activation(prob[:, within], gap[:], ACT.Sigmoid, scale=-1.0)
+            nc.sync.dma_start(out=out[:, stored], in_=prob[:])

@@ -20,8 +20,8 @@ PACK = 4
 HALF = S // 2
 LIST_ROWS = 16
 BANK = 512
-LAST_CHUNKS = (2816, 960, 320)
-VECTOR_ROUNDS = (1856, 672, 0)
+LAST_CHUNKS = (512, 2496, 832, 256)
+VECTOR_ROUNDS = (0, 1664, 560, 0)
 SCORE_PIECES = (256, 256, 128, 128, 128, 64, 64)
 VECTOR_BANKS = (3, 5)
 WIN_PIECES = (256, 256)
@@ -49,15 +49,16 @@ def tile_picked_ranknet_sigmoid_e_kernel(tc, xT, w1_words, w1_scales, offs, win,
         w_codes = keep.tile([P, N], U32, name="w_codes", align_bytes=64)
         w_scale = keep.tile([P, N], U8, name="w_scale", align_bytes=64)
         rows01 = keep.tile([P, 2, T], F32, name="rows01")
-        rows = {j: keep.tile([P, T], F32, name="rows%d" % j) for j in (2, 3)}
+        rows23 = keep.tile([P, 2 * T], F32, name="rows23")
+        row2, row3 = rows23[:, :T], rows23[:, T:]
         last_bf = keep.tile([P, T], BF16, name="last_bf")
         x_rows = xT.rearrange("(p j) t -> p j t", j=PACK)
 
         nc.sync.dma_start(out=rows01[:], in_=x_rows[:, 0:2, :])
         nc.sync.dma_start(offs_sb[:], offs)
-        nc.sync.dma_start(out=rows[2][:], in_=x_rows[:, 2, :])
-        for cols in spans(LAST_CHUNKS):
-            nc.sync.dma_start(out=rows[3][:, cols], in_=x_rows[:, 3, cols])
+        x_rows23 = x_rows[:, 2:4, :].rearrange("p j t -> p (j t)")
+        for cols in spans((T + LAST_CHUNKS[0],) + LAST_CHUNKS[1:]):
+            nc.sync.dma_start(out=rows23[:, cols], in_=x_rows23[:, cols])
         nc.sync.dma_start(out=w_codes[:].bitcast(I32), in_=w1_words[0].rearrange("p n t -> p (n t)").bitcast(I32))
         nc.vector.memset(w_scale[:].bitcast(I32), 0)
         for q in range(4):
@@ -80,17 +81,17 @@ def tile_picked_ranknet_sigmoid_e_kernel(tc, xT, w1_words, w1_scales, offs, win,
         nc.scalar.copy(words[0], pair_words[:, 1, :].unsqueeze(2).to_broadcast([P, HALF, 2]))
         for j in (0, 1):
             nc.vector.tensor_copy(pairs[:, 0, :, j], rows01[:, j, :].indirect(halves[1]))
-        nc.vector.tensor_copy(pairs[:, 1, :, 0], rows[2][:].indirect(halves[1]))
+        nc.vector.tensor_copy(pairs[:, 1, :, 0], row2.indirect(halves[1]))
         nc.scalar.copy(words[1], pair_words.rearrange("p u n -> p n u"))
-        nc.vector.tensor_copy(picked[0][:, :, 2], rows[2][:].indirect(halves[0]))
+        nc.vector.tensor_copy(picked[0][:, :, 2], row2.indirect(halves[0]))
         for cols, by_vector in zip(spans(LAST_CHUNKS), VECTOR_ROUNDS):
             split = cols.stop - by_vector
             if split > cols.start:
-                nc.scalar.activation(last_bf[:, cols.start : split], rows[3][:, cols.start : split], ACT.Copy)
+                nc.scalar.activation(last_bf[:, cols.start : split], row3[:, cols.start : split], ACT.Copy)
             if by_vector > 0:
-                nc.vector.tensor_copy(last_bf[:, split : cols.stop], rows[3][:, split : cols.stop])
+                nc.vector.tensor_copy(last_bf[:, split : cols.stop], row3[:, split : cols.stop])
         nc.scalar.activation(picked[1][:, :, 3], last_bf[:].indirect(halves[1]), ACT.Copy)
-        nc.vector.tensor_copy(picked[0][:, :, 3], rows[3][:].indirect(halves[0]))
+        nc.vector.tensor_copy(picked[0][:, :, 3], row3.indirect(halves[0]))
 
         banks = []
         for i, cols in enumerate(spans(SCORE_PIECES)):

@@ -20,8 +20,9 @@ PACK = 4
 HALF = S // 2
 LIST_ROWS = 16
 BANK = 512
-LAST_CHUNKS = (512, 2496, 832, 256)
-VECTOR_ROUNDS = (0, 1664, 560, 0)
+LAST_CHUNKS = (928, 2176, 768, 224)
+VECTOR_ROUNDS = (0, 1536, 512, 0)
+WEAVE_PIECES = (256, 256)
 SCORE_PIECES = (256, 256, 128, 128, 128, 64, 64)
 VECTOR_BANKS = (3, 5)
 WIN_PIECES = (256, 256)
@@ -73,17 +74,17 @@ def tile_picked_ranknet_sigmoid_e_kernel(tc, xT, w1_words, w1_scales, offs, win,
         y = keep.tile([P, S], F32, name="y")
         halves = [offs_sb[:, list_cols(slice(h * HALF, (h + 1) * HALF))] for h in range(2)]
 
-        pairs = keep.tile([P, 2, HALF, 2], BF16, name="pairs")
-        pair_words = pairs[:].rearrange("p u n e -> p u (n e)").bitcast(U32)
+        pairs = [keep.tile([P, 2, HALF, 2], BF16, name="pairs%d" % h) for h in range(2)]
+        pair_words = [pairs[h][:].rearrange("p u n e -> p u (n e)").bitcast(U32) for h in range(2)]
         words = [picked[h][:].rearrange("p n j -> p (n j)").bitcast(U32).rearrange("p (n u) -> p n u", u=2) for h in range(2)]
         for j in (0, 1):
-            nc.vector.tensor_copy(pairs[:, 1, :, j], rows01[:, j, :].indirect(halves[0]))
-        nc.scalar.copy(words[0], pair_words[:, 1, :].unsqueeze(2).to_broadcast([P, HALF, 2]))
+            nc.vector.tensor_copy(pairs[1][:, 1, :, j], rows01[:, j, :].indirect(halves[1]))
+        nc.scalar.copy(pair_words[1][:, 0, :], pair_words[1][:, 1, :])
         for j in (0, 1):
-            nc.vector.tensor_copy(pairs[:, 0, :, j], rows01[:, j, :].indirect(halves[1]))
-        nc.vector.tensor_copy(pairs[:, 1, :, 0], row2.indirect(halves[1]))
-        nc.scalar.copy(words[1], pair_words.rearrange("p u n -> p n u"))
-        nc.vector.tensor_copy(picked[0][:, :, 2], row2.indirect(halves[0]))
+            nc.vector.tensor_copy(pairs[0][:, 0, :, j], rows01[:, j, :].indirect(halves[0]))
+        nc.vector.tensor_copy(pairs[1][:, 1, :, 0], row2.indirect(halves[1]))
+        nc.scalar.copy(words[1], pair_words[1].rearrange("p u n -> p n u"))
+        nc.vector.tensor_copy(pairs[0][:, 1, :, 0], row2.indirect(halves[0]))
         for cols, by_vector in zip(spans(LAST_CHUNKS), VECTOR_ROUNDS):
             split = cols.stop - by_vector
             if split > cols.start:
@@ -91,7 +92,9 @@ def tile_picked_ranknet_sigmoid_e_kernel(tc, xT, w1_words, w1_scales, offs, win,
             if by_vector > 0:
                 nc.vector.tensor_copy(last_bf[:, split : cols.stop], row3[:, split : cols.stop])
         nc.scalar.activation(picked[1][:, :, 3], last_bf[:].indirect(halves[1]), ACT.Copy)
-        nc.vector.tensor_copy(picked[0][:, :, 3], row3.indirect(halves[0]))
+        nc.vector.tensor_copy(pairs[0][:, 1, :, 1], row3.indirect(halves[0]))
+        for entries in spans(WEAVE_PIECES):
+            nc.vector.tensor_copy(words[0][:, entries, :].bitcast(I32), pair_words[0][:, :, entries].bitcast(I32).rearrange("p u n -> p n u"))
 
         banks = []
         for i, cols in enumerate(spans(SCORE_PIECES)):

@@ -20,8 +20,8 @@ PACK = 4
 HALF = S // 2
 LIST_ROWS = 16
 BANK = 512
-LAST_CHUNKS = (928, 2176, 768, 224)
-VECTOR_ROUNDS = (0, 1536, 512, 0)
+LAST_CHUNKS = (896, 2176, 768, 256)
+VECTOR_ROUNDS = (0, 1536, 480, 0)
 WEAVE_PIECES = (256, 256)
 SCORE_PIECES = (256, 256, 128, 128, 128, 64, 64)
 VECTOR_BANKS = (3, 5)

@@ -20,13 +20,13 @@ PACK = 4
 HALF = S // 2
 LIST_ROWS = 16
 BANK = 512
-LAST_CHUNKS = (896, 2176, 768, 256)
-VECTOR_ROUNDS = (0, 1536, 480, 0)
+LAY_PIECES = (256, 256)
 WEAVE_PIECES = (256, 256)
 SCORE_PIECES = (256, 256, 128, 128, 128, 64, 64)
 VECTOR_BANKS = (3, 5)
-WIN_PIECES = (256, 256)
-STORES = ((160,), (160,), (128, 64))
+VECTOR_WINS = (128,)
+SCALAR_WINS = (192, 192)
+STORES = ((128,), (192,), (128, 64))
 
 
 def spans(widths, first=0):
@@ -50,16 +50,14 @@ def tile_picked_ranknet_sigmoid_e_kernel(tc, xT, w1_words, w1_scales, offs, win,
         w_codes = keep.tile([P, N], U32, name="w_codes", align_bytes=64)
         w_scale = keep.tile([P, N], U8, name="w_scale", align_bytes=64)
         rows01 = keep.tile([P, 2, T], F32, name="rows01")
-        rows23 = keep.tile([P, 2 * T], F32, name="rows23")
-        row2, row3 = rows23[:, :T], rows23[:, T:]
-        last_bf = keep.tile([P, T], BF16, name="last_bf")
+        row2 = keep.tile([P, T], F32, name="row2")
+        row3 = keep.tile([P, T], F32, name="row3")
         x_rows = xT.rearrange("(p j) t -> p j t", j=PACK)
 
         nc.sync.dma_start(out=rows01[:], in_=x_rows[:, 0:2, :])
         nc.sync.dma_start(offs_sb[:], offs)
-        x_rows23 = x_rows[:, 2:4, :].rearrange("p j t -> p (j t)")
-        for cols in spans((T + LAST_CHUNKS[0],) + LAST_CHUNKS[1:]):
-            nc.sync.dma_start(out=rows23[:, cols], in_=x_rows23[:, cols])
+        nc.sync.dma_start(out=row2[:], in_=x_rows[:, 2, :])
+        nc.sync.dma_start(out=row3[:], in_=x_rows[:, 3, :])
         nc.sync.dma_start(out=w_codes[:].bitcast(I32), in_=w1_words[0].rearrange("p n t -> p (n t)").bitcast(I32))
         nc.vector.memset(w_scale[:].bitcast(I32), 0)
         for q in range(4):
@@ -70,31 +68,37 @@ def tile_picked_ranknet_sigmoid_e_kernel(tc, xT, w1_words, w1_scales, offs, win,
         nc.sync.dma_start(win_sb[:], win)
         nc.sync.dma_start(lose_sb[:], lose)
 
-        picked = [keep.tile([P, HALF, PACK], BF16, name="picked%d" % h, align_bytes=64) for h in range(2)]
-        y = keep.tile([P, S], F32, name="y")
-        halves = [offs_sb[:, list_cols(slice(h * HALF, (h + 1) * HALF))] for h in range(2)]
+        warm_in = keep.tile([P, 1], F32, name="warm_in")
+        warm_out = keep.tile([P, 1], F32, name="warm_out")
+        nc.vector.memset(warm_in[:], 0.0)
+        nc.scalar.activation(warm_out[:], warm_in[:], ACT.Sigmoid)
 
-        pairs = [keep.tile([P, 2, HALF, 2], BF16, name="pairs%d" % h) for h in range(2)]
-        pair_words = [pairs[h][:].rearrange("p u n e -> p u (n e)").bitcast(U32) for h in range(2)]
+        picked = [keep.tile([P, HALF, PACK], BF16, name="picked%d" % h, align_bytes=64) for h in range(2)]
         words = [picked[h][:].rearrange("p n j -> p (n j)").bitcast(U32).rearrange("p (n u) -> p n u", u=2) for h in range(2)]
+        y = keep.tile([P, S], F32, name="y")
+        halves = [slice(h * HALF, (h + 1) * HALF) for h in range(2)]
+        lists = [offs_sb[:, list_cols(half)] for half in halves]
+
+        early_pairs = keep.tile([P, HALF, 2], BF16, name="early_pairs")
+        late_pairs = keep.tile([P, 2, HALF, 2], BF16, name="late_pairs")
+        late_words = late_pairs[:].rearrange("p u n e -> p u (n e)").bitcast(U32)
+        dense3 = keep.tile([P, HALF], BF16, name="dense3")
+
         for j in (0, 1):
-            nc.vector.tensor_copy(pairs[1][:, 1, :, j], rows01[:, j, :].indirect(halves[1]))
-        nc.scalar.copy(pair_words[1][:, 0, :], pair_words[1][:, 1, :])
+            nc.vector.tensor_copy(early_pairs[:, :, j], rows01[:, j, :].indirect(lists[0]))
+        nc.scalar.copy(words[0][:, :, 0], early_pairs[:].rearrange("p n e -> p (n e)").bitcast(U32))
         for j in (0, 1):
-            nc.vector.tensor_copy(pairs[0][:, 0, :, j], rows01[:, j, :].indirect(halves[0]))
-        nc.vector.tensor_copy(pairs[1][:, 1, :, 0], row2.indirect(halves[1]))
-        nc.scalar.copy(words[1], pair_words[1].rearrange("p u n -> p n u"))
-        nc.vector.tensor_copy(pairs[0][:, 1, :, 0], row2.indirect(halves[0]))
-        for cols, by_vector in zip(spans(LAST_CHUNKS), VECTOR_ROUNDS):
-            split = cols.stop - by_vector
-            if split > cols.start:
-                nc.scalar.activation(last_bf[:, cols.start : split], row3[:, cols.start : split], ACT.Copy)
-            if by_vector > 0:
-                nc.vector.tensor_copy(last_bf[:, split : cols.stop], row3[:, split : cols.stop])
-        nc.scalar.activation(picked[1][:, :, 3], last_bf[:].indirect(halves[1]), ACT.Copy)
-        nc.vector.tensor_copy(pairs[0][:, 1, :, 1], row3.indirect(halves[0]))
+            nc.vector.tensor_copy(late_pairs[:, 0, :, j], rows01[:, j, :].indirect(lists[1]))
+        nc.vector.tensor_copy(picked[0][:, :, 2], row2[:].indirect(lists[0]))
+        nc.vector.tensor_copy(late_pairs[:, 1, :, 0], row2[:].indirect(lists[1]))
+
+        nc.vector.tensor_copy(late_pairs[:, 1, :, 1], row3[:].indirect(lists[1]))
+        for entries in spans(LAY_PIECES):
+            nc.scalar.activation(dense3[:, entries], row3[:].indirect(offs_sb[:, list_cols(entries)]), ACT.Copy)
+        for entries in spans(LAY_PIECES):
+            nc.vector.tensor_copy(picked[0][:, entries, 3], dense3[:, entries])
         for entries in spans(WEAVE_PIECES):
-            nc.vector.tensor_copy(words[0][:, entries, :].bitcast(I32), pair_words[0][:, :, entries].bitcast(I32).rearrange("p u n -> p n u"))
+            nc.scalar.copy(words[1][:, entries, :], late_words[:, :, entries].rearrange("p u n -> p n u"))
 
         banks = []
         for i, cols in enumerate(spans(SCORE_PIECES)):
@@ -125,8 +129,10 @@ def tile_picked_ranknet_sigmoid_e_kernel(tc, xT, w1_words, w1_scales, offs, win,
                 nc.scalar.activation(y[:, cols], banks[i], ACT.Copy)
 
         y_win = keep.tile([P, V], F32, name="y_win")
-        for cols in spans(WIN_PIECES):
+        for cols in spans(VECTOR_WINS):
             nc.vector.tensor_copy(y_win[:, cols], y[:].indirect(win_sb[:, list_cols(cols)]))
+        for cols in spans(SCALAR_WINS, sum(VECTOR_WINS)):
+            nc.scalar.activation(y_win[:, cols], y[:].indirect(win_sb[:, list_cols(cols)]), ACT.Copy)
         for stored, widths in zip(spans([sum(widths) for widths in STORES]), STORES):
             prob = keep.tile([P, sum(widths)], F32, name="prob%d" % stored.start)
             for cols, within in zip(spans(widths, stored.start), spans(widths)):

@@ -24,9 +24,11 @@ LAY_PIECES = (256, 256)
 WEAVE_PIECES = (256, 256)
 SCORE_PIECES = (256, 256, 128, 128, 128, 64, 64)
 VECTOR_BANKS = (3, 5)
-VECTOR_WINS = (128,)
-SCALAR_WINS = (192, 192)
-STORES = ((128,), (192,), (128, 64))
+WIN_PIECES = (64, 128, 96, 96, 128)
+VECTOR_WINS = (0, 3)
+GAP_PIECES = (64, 128, 160, 96, 64)
+SIGMOID_PIECES = (192, 160, 96, 64)
+STORE_PIECES = (192, 160, 160)
 
 
 def spans(widths, first=0):
@@ -129,14 +131,17 @@ def tile_picked_ranknet_sigmoid_e_kernel(tc, xT, w1_words, w1_scales, offs, win,
                 nc.scalar.activation(y[:, cols], banks[i], ACT.Copy)
 
         y_win = keep.tile([P, V], F32, name="y_win")
-        for cols in spans(VECTOR_WINS):
-            nc.vector.tensor_copy(y_win[:, cols], y[:].indirect(win_sb[:, list_cols(cols)]))
-        for cols in spans(SCALAR_WINS, sum(VECTOR_WINS)):
-            nc.scalar.activation(y_win[:, cols], y[:].indirect(win_sb[:, list_cols(cols)]), ACT.Copy)
-        for stored, widths in zip(spans([sum(widths) for widths in STORES]), STORES):
-            prob = keep.tile([P, sum(widths)], F32, name="prob%d" % stored.start)
-            for cols, within in zip(spans(widths, stored.start), spans(widths)):
-                gap = keep.tile([P, cols.stop - cols.start], F32, name="gap%d" % cols.start)
-                nc.vector.tensor_tensor(gap[:], y[:].indirect(lose_sb[:, list_cols(cols)]), y_win[:, cols], ALU.subtract)
-                nc.scalar.activation(prob[:, within], gap[:], ACT.Sigmoid, scale=-1.0)
-            nc.sync.dma_start(out=out[:, stored], in_=prob[:])
+        gap = keep.tile([P, V], F32, name="gap")
+        prob = keep.tile([P, V], F32, name="prob")
+        for i, cols in enumerate(spans(WIN_PIECES)):
+            winners = y[:].indirect(win_sb[:, list_cols(cols)])
+            if i in VECTOR_WINS:
+                nc.vector.tensor_copy(y_win[:, cols], winners)
+            else:
+                nc.scalar.activation(y_win[:, cols], winners, ACT.Copy)
+        for cols in spans(GAP_PIECES):
+            nc.vector.tensor_tensor(gap[:, cols], y[:].indirect(lose_sb[:, list_cols(cols)]), y_win[:, cols], ALU.subtract)
+        for cols in spans(SIGMOID_PIECES):
+            nc.scalar.activation(prob[:, cols], gap[:, cols], ACT.Sigmoid, scale=-1.0)
+        for cols in spans(STORE_PIECES):
+            nc.sync.dma_start(out=out[:, cols], in_=prob[:, cols])

@@ -20,10 +20,13 @@ PACK = 4
 HALF = S // 2
 LIST_ROWS = 16
 BANK = 512
-LAY_PIECES = (256, 256)
+DENSE_PIECES = (128, 192, 192)
+GPSIMD_LAYS = 128
+LAY_PIECES = (192, 192)
 WEAVE_PIECES = (256, 256)
-SCORE_PIECES = (256, 256, 128, 128, 128, 64, 64)
-VECTOR_BANKS = (3, 5)
+SCORE_PIECES = (128,) * 8
+VECTOR_BANKS = (2, 4)
+BANK_PIECES = (256, 256, 128, 128, 128, 128)
 WIN_PIECES = (64, 128, 96, 96, 128)
 VECTOR_WINS = (0, 3)
 GAP_PIECES = (64, 128, 160, 96, 64)
@@ -81,29 +84,27 @@ def tile_picked_ranknet_sigmoid_e_kernel(tc, xT, w1_words, w1_scales, offs, win,
         halves = [slice(h * HALF, (h + 1) * HALF) for h in range(2)]
         lists = [offs_sb[:, list_cols(half)] for half in halves]
 
-        early_pairs = keep.tile([P, HALF, 2], BF16, name="early_pairs")
-        late_pairs = keep.tile([P, 2, HALF, 2], BF16, name="late_pairs")
-        late_words = late_pairs[:].rearrange("p u n e -> p u (n e)").bitcast(U32)
+        pairs = [keep.tile([P, 2, HALF, 2], BF16, name="pairs%d" % h) for h in range(2)]
+        pair_words = [pairs[h][:].rearrange("p u n e -> p u (n e)").bitcast(U32) for h in range(2)]
         dense3 = keep.tile([P, HALF], BF16, name="dense3")
 
         for j in (0, 1):
-            nc.vector.tensor_copy(early_pairs[:, :, j], rows01[:, j, :].indirect(lists[0]))
-        nc.scalar.copy(words[0][:, :, 0], early_pairs[:].rearrange("p n e -> p (n e)").bitcast(U32))
+            nc.vector.tensor_copy(pairs[0][:, 1, :, j], rows01[:, j, :].indirect(lists[0]))
+        nc.scalar.copy(pair_words[0][:, 0, :], pair_words[0][:, 1, :])
         for j in (0, 1):
-            nc.vector.tensor_copy(late_pairs[:, 0, :, j], rows01[:, j, :].indirect(lists[1]))
-        nc.vector.tensor_copy(picked[0][:, :, 2], row2[:].indirect(lists[0]))
-        nc.vector.tensor_copy(late_pairs[:, 1, :, 0], row2[:].indirect(lists[1]))
+            nc.vector.tensor_copy(pairs[1][:, 0, :, j], rows01[:, j, :].indirect(lists[1]))
+        nc.vector.tensor_copy(pairs[0][:, 1, :, 0], row2[:].indirect(lists[0]))
+        nc.scalar.copy(words[0], pair_words[0].rearrange("p u n -> p n u"))
+        nc.vector.tensor_copy(pairs[1][:, 1, :, 0], row2[:].indirect(lists[1]))
 
-        nc.vector.tensor_copy(late_pairs[:, 1, :, 1], row3[:].indirect(lists[1]))
-        for entries in spans(LAY_PIECES):
+        nc.vector.tensor_copy(pairs[1][:, 1, :, 1], row3[:].indirect(lists[1]))
+        for entries in spans(DENSE_PIECES):
             nc.scalar.activation(dense3[:, entries], row3[:].indirect(offs_sb[:, list_cols(entries)]), ACT.Copy)
-        for entries in spans(LAY_PIECES):
-            nc.vector.tensor_copy(picked[0][:, entries, 3], dense3[:, entries])
+        nc.gpsimd.tensor_copy(picked[0][:, :GPSIMD_LAYS, 3], dense3[:, :GPSIMD_LAYS])
         for entries in spans(WEAVE_PIECES):
-            nc.scalar.copy(words[1][:, entries, :], late_words[:, :, entries].rearrange("p u n -> p n u"))
+            nc.scalar.copy(words[1][:, entries, :], pair_words[1][:, :, entries].rearrange("p u n -> p n u"))
 
-        banks = []
-        for i, cols in enumerate(spans(SCORE_PIECES)):
+        def score(i, cols):
             width = cols.stop - cols.start
             h, first = divmod(cols.start, HALF)
             codes = keep.tile([P, width], U32, name="codes%d" % i, align_bytes=64)
@@ -113,9 +114,9 @@ def tile_picked_ranknet_sigmoid_e_kernel(tc, xT, w1_words, w1_scales, offs, win,
                 scales=scales[:],
                 in_=picked[h][:, first : first + width, :].rearrange("p n j -> p (n j)"),
             )
-            bank = psum.tile([P, BANK], F32, name="bank%d" % i)
+            b = max(b for b, held in enumerate(bank_cols) if held.start <= cols.start)
             nc.tensor.matmul_mx(
-                out=bank[:, :width],
+                out=banks[b][:, cols.start - bank_cols[b].start : cols.stop - bank_cols[b].start],
                 lhsT=w_codes[:].bitcast(FP8X4),
                 lhsT_scale=w_scale[:],
                 rhs=codes[:].bitcast(FP8X4),
@@ -123,12 +124,19 @@ def tile_picked_ranknet_sigmoid_e_kernel(tc, xT, w1_words, w1_scales, offs, win,
                 start=True,
                 stop=True,
             )
-            banks.append(bank[:, :width])
+
+        bank_cols = spans(BANK_PIECES)
+        banks = [psum.tile([P, BANK], F32, name="bank%d" % b) for b in range(len(bank_cols))]
+        lays = spans(LAY_PIECES, GPSIMD_LAYS)
         for i, cols in enumerate(spans(SCORE_PIECES)):
-            if i in VECTOR_BANKS:
-                nc.vector.tensor_copy(y[:, cols], banks[i])
+            if i < len(lays):
+                nc.vector.tensor_copy(picked[0][:, lays[i], 3], dense3[:, lays[i]])
+            score(i, cols)
+        for b, cols in enumerate(bank_cols):
+            if b in VECTOR_BANKS:
+                nc.vector.tensor_copy(y[:, cols], banks[b][:, : BANK_PIECES[b]])
             else:
-                nc.scalar.activation(y[:, cols], banks[i], ACT.Copy)
+                nc.scalar.activation(y[:, cols], banks[b][:, : BANK_PIECES[b]], ACT.Copy)
 
         y_win = keep.tile([P, V], F32, name="y_win")
         gap = keep.tile([P, V], F32, name="gap")

@@ -20,10 +20,10 @@ PACK = 4
 HALF = S // 2
 LIST_ROWS = 16
 BANK = 512
-DENSE_PIECES = (128, 192, 192)
+DENSE_PIECES = (128, 128, 128, 128)
 GPSIMD_LAYS = 128
-LAY_PIECES = (192, 192)
-WEAVE_PIECES = (256, 256)
+LAYS_BEFORE = ((128, 128), (128,))
+WEAVE_PIECES = (256, 128, 128)
 SCORE_PIECES = (128,) * 8
 VECTOR_BANKS = (2, 4)
 BANK_PIECES = (256, 256, 128, 128, 128, 128)
@@ -127,10 +127,12 @@ def tile_picked_ranknet_sigmoid_e_kernel(tc, xT, w1_words, w1_scales, offs, win,
 
         bank_cols = spans(BANK_PIECES)
         banks = [psum.tile([P, BANK], F32, name="bank%d" % b) for b in range(len(bank_cols))]
-        lays = spans(LAY_PIECES, GPSIMD_LAYS)
+        laid = GPSIMD_LAYS
         for i, cols in enumerate(spans(SCORE_PIECES)):
-            if i < len(lays):
-                nc.vector.tensor_copy(picked[0][:, lays[i], 3], dense3[:, lays[i]])
+            if i < len(LAYS_BEFORE):
+                for entries in spans(LAYS_BEFORE[i], laid):
+                    nc.vector.tensor_copy(picked[0][:, entries, 3], dense3[:, entries])
+                laid = laid + sum(LAYS_BEFORE[i])
             score(i, cols)
         for b, cols in enumerate(bank_cols):
             if b in VECTOR_BANKS:

@@ -27,11 +27,12 @@ WEAVE_PIECES = (256, 128, 128)
 SCORE_PIECES = (128,) * 8
 VECTOR_BANKS = (2, 4)
 BANK_PIECES = (256, 256, 128, 128, 128, 128)
-WIN_PIECES = (64, 128, 96, 96, 128)
-VECTOR_WINS = (0, 3)
-GAP_PIECES = (64, 128, 160, 96, 64)
-SIGMOID_PIECES = (192, 160, 96, 64)
-STORE_PIECES = (192, 160, 160)
+WIN_PIECES = (64, 192, 256)
+VECTOR_WINS = (1,)
+GAP_PIECES = (64, 192, 128)
+SCALAR_LOSERS = 128
+SIGMOID_PIECES = (64, 192, 128, 128)
+STORE_PIECES = (256, 128, 128)
 
 
 def spans(widths, first=0):
@@ -149,8 +150,12 @@ def tile_picked_ranknet_sigmoid_e_kernel(tc, xT, w1_words, w1_scales, offs, win,
                 nc.vector.tensor_copy(y_win[:, cols], winners)
             else:
                 nc.scalar.activation(y_win[:, cols], winners, ACT.Copy)
+        tail = slice(V - SCALAR_LOSERS, V)
+        y_lose = keep.tile([P, SCALAR_LOSERS], F32, name="y_lose")
+        nc.scalar.activation(y_lose[:], y[:].indirect(lose_sb[:, list_cols(tail)]), ACT.Copy)
         for cols in spans(GAP_PIECES):
             nc.vector.tensor_tensor(gap[:, cols], y[:].indirect(lose_sb[:, list_cols(cols)]), y_win[:, cols], ALU.subtract)
+        nc.vector.tensor_tensor(gap[:, tail], y_lose[:], y_win[:, tail], ALU.subtract)
         for cols in spans(SIGMOID_PIECES):
             nc.scalar.activation(prob[:, cols], gap[:, cols], ACT.Sigmoid, scale=-1.0)
         for cols in spans(STORE_PIECES):

@@ -32,7 +32,7 @@ VECTOR_WINS = (1,)
 GAP_PIECES = (64, 192, 128)
 SCALAR_LOSERS = 128
 SIGMOID_PIECES = (64, 192, 128, 128)
-STORE_PIECES = (256, 128, 128)
+STORE_PIECES = (64, 192, 256)
 
 
 def spans(widths, first=0):

@@ -17,16 +17,17 @@ ALU = mybir.AluOpType
 
 P = 128
 PACK = 4
-HALF = S // 2
 LIST_ROWS = 16
 BANK = 512
-DENSE_PIECES = (128, 128, 128, 128)
-GPSIMD_LAYS = 128
-LAYS_BEFORE = ((128, 128), (128,))
-WEAVE_PIECES = (256, 128, 128)
-SCORE_PIECES = (128,) * 8
-VECTOR_BANKS = (2, 4)
-BANK_PIECES = (256, 256, 128, 128, 128, 128)
+HALF = S // 2
+GATHER_PIECES = (128, 128, 128, 128)
+VECTOR_WEAVES = 256
+SCALAR_WEAVES = (128, 128)
+PIECE = 128
+SCORE_ORDER = (0, 1, 2, 4, 5, 3, 6, 7)
+BANK_PIECES = (256, 256, 256, 128, 128)
+BANK_ORDER = (0, 2, 1, 3, 4)
+VECTOR_BANKS = (1, 4)
 WIN_PIECES = (64, 192, 256)
 VECTOR_WINS = (1,)
 GAP_PIECES = (64, 192, 128)
@@ -44,6 +45,10 @@ def list_cols(entries):
     return slice(entries.start // LIST_ROWS, entries.stop // LIST_ROWS)
 
 
+def as_words(pairs, dtype):
+    return pairs.rearrange("p n e -> p (n e)").bitcast(dtype)
+
+
 def tile_picked_ranknet_sigmoid_e_kernel(tc, xT, w1_words, w1_scales, offs, win, lose, out):
     nc = tc.nc
     with ExitStack() as ctx:
@@ -55,9 +60,9 @@ def tile_picked_ranknet_sigmoid_e_kernel(tc, xT, w1_words, w1_scales, offs, win,
         lose_sb = keep.tile([P, V // LIST_ROWS], U16, name="lose_sb")
         w_codes = keep.tile([P, N], U32, name="w_codes", align_bytes=64)
         w_scale = keep.tile([P, N], U8, name="w_scale", align_bytes=64)
-        rows01 = keep.tile([P, 2, T], F32, name="rows01")
-        row2 = keep.tile([P, T], F32, name="row2")
-        row3 = keep.tile([P, T], F32, name="row3")
+        rows01 = keep.tile([P, 2, T], F32, name="rows01", align_bytes=256)
+        row2 = keep.tile([P, T], F32, name="row2", align_bytes=256)
+        row3 = keep.tile([P, T], F32, name="row3", align_bytes=256)
         x_rows = xT.rearrange("(p j) t -> p j t", j=PACK)
 
         nc.sync.dma_start(out=rows01[:], in_=x_rows[:, 0:2, :])
@@ -79,41 +84,49 @@ def tile_picked_ranknet_sigmoid_e_kernel(tc, xT, w1_words, w1_scales, offs, win,
         nc.vector.memset(warm_in[:], 0.0)
         nc.scalar.activation(warm_out[:], warm_in[:], ACT.Sigmoid)
 
-        picked = [keep.tile([P, HALF, PACK], BF16, name="picked%d" % h, align_bytes=64) for h in range(2)]
-        words = [picked[h][:].rearrange("p n j -> p (n j)").bitcast(U32).rearrange("p (n u) -> p n u", u=2) for h in range(2)]
         y = keep.tile([P, S], F32, name="y")
-        halves = [slice(h * HALF, (h + 1) * HALF) for h in range(2)]
-        lists = [offs_sb[:, list_cols(half)] for half in halves]
+        picked = keep.tile([P, S, PACK], BF16, name="picked", align_bytes=64)
+        first, second = slice(0, HALF), slice(HALF, S)
 
-        pairs = [keep.tile([P, 2, HALF, 2], BF16, name="pairs%d" % h) for h in range(2)]
-        pair_words = [pairs[h][:].rearrange("p u n e -> p u (n e)").bitcast(U32) for h in range(2)]
-        dense3 = keep.tile([P, HALF], BF16, name="dense3")
+        def offsets(entries):
+            return offs_sb[:, list_cols(entries)]
+
+        def words(entries, dtype):
+            return as_words(picked[:, entries, :], dtype).rearrange("p (n u) -> p n u", u=2)
+
+        low = keep.tile([P, HALF, 2], BF16, name="low")
+        pairs = keep.tile([P, 2, HALF, 2], BF16, name="pairs")
+
+        def weave(copy, dtype, entries):
+            held = slice(entries.start - HALF, entries.stop - HALF)
+            copy(words(entries, dtype), pairs[:].rearrange("p u n e -> p u (n e)").bitcast(dtype)[:, :, held].rearrange("p u n -> p n u"))
 
         for j in (0, 1):
-            nc.vector.tensor_copy(pairs[0][:, 1, :, j], rows01[:, j, :].indirect(lists[0]))
-        nc.scalar.copy(pair_words[0][:, 0, :], pair_words[0][:, 1, :])
+            nc.vector.tensor_copy(low[:, :, j], rows01[:, j, :].indirect(offsets(first)))
+        nc.scalar.copy(words(first, U32)[:, :, 0], as_words(low[:], U32))
         for j in (0, 1):
-            nc.vector.tensor_copy(pairs[1][:, 0, :, j], rows01[:, j, :].indirect(lists[1]))
-        nc.vector.tensor_copy(pairs[0][:, 1, :, 0], row2[:].indirect(lists[0]))
-        nc.scalar.copy(words[0], pair_words[0].rearrange("p u n -> p n u"))
-        nc.vector.tensor_copy(pairs[1][:, 1, :, 0], row2[:].indirect(lists[1]))
+            nc.vector.tensor_copy(pairs[:, 0, :, j], rows01[:, j, :].indirect(offsets(second)))
+        nc.vector.tensor_copy(pairs[:, 1, :, 0], row2[:].indirect(offsets(second)))
+        nc.scalar.activation(picked[:, first, 2], row2[:].indirect(offsets(first)), ACT.Copy)
 
-        nc.vector.tensor_copy(pairs[1][:, 1, :, 1], row3[:].indirect(lists[1]))
-        for entries in spans(DENSE_PIECES):
-            nc.scalar.activation(dense3[:, entries], row3[:].indirect(offs_sb[:, list_cols(entries)]), ACT.Copy)
-        nc.gpsimd.tensor_copy(picked[0][:, :GPSIMD_LAYS, 3], dense3[:, :GPSIMD_LAYS])
-        for entries in spans(WEAVE_PIECES):
-            nc.scalar.copy(words[1][:, entries, :], pair_words[1][:, :, entries].rearrange("p u n -> p n u"))
+        nc.vector.tensor_copy(pairs[:, 1, :, 1], row3[:].indirect(offsets(second)))
+        for entries in spans(GATHER_PIECES):
+            nc.scalar.activation(picked[:, entries, 3], row3[:].indirect(offsets(entries)), ACT.Copy)
+        for entries in spans(SCALAR_WEAVES, HALF + VECTOR_WEAVES):
+            weave(nc.scalar.copy, U32, entries)
 
-        def score(i, cols):
-            width = cols.stop - cols.start
-            h, first = divmod(cols.start, HALF)
-            codes = keep.tile([P, width], U32, name="codes%d" % i, align_bytes=64)
-            scales = keep.tile([P, width], U8, name="scales%d" % i, align_bytes=64)
+        bank_cols = spans(BANK_PIECES)
+        banks = [psum.tile([P, BANK], F32, name="bank%d" % b) for b in range(len(bank_cols))]
+        for i in SCORE_ORDER:
+            cols = slice(i * PIECE, (i + 1) * PIECE)
+            if i == 1:
+                weave(nc.vector.tensor_copy, I32, slice(HALF, HALF + VECTOR_WEAVES))
+            codes = keep.tile([P, PIECE], U32, name="codes%d" % i, align_bytes=64)
+            scales = keep.tile([P, PIECE], U8, name="scales%d" % i, align_bytes=64)
             nc.vector.quantize_mx(
                 out=codes[:].bitcast(FP8X4),
                 scales=scales[:],
-                in_=picked[h][:, first : first + width, :].rearrange("p n j -> p (n j)"),
+                in_=picked[:, cols, :].rearrange("p n j -> p (n j)"),
             )
             b = max(b for b, held in enumerate(bank_cols) if held.start <= cols.start)
             nc.tensor.matmul_mx(
@@ -125,17 +138,8 @@ def tile_picked_ranknet_sigmoid_e_kernel(tc, xT, w1_words, w1_scales, offs, win,
                 start=True,
                 stop=True,
             )
-
-        bank_cols = spans(BANK_PIECES)
-        banks = [psum.tile([P, BANK], F32, name="bank%d" % b) for b in range(len(bank_cols))]
-        laid = GPSIMD_LAYS
-        for i, cols in enumerate(spans(SCORE_PIECES)):
-            if i < len(LAYS_BEFORE):
-                for entries in spans(LAYS_BEFORE[i], laid):
-                    nc.vector.tensor_copy(picked[0][:, entries, 3], dense3[:, entries])
-                laid = laid + sum(LAYS_BEFORE[i])
-            score(i, cols)
-        for b, cols in enumerate(bank_cols):
+        for b in BANK_ORDER:
+            cols = bank_cols[b]
             if b in VECTOR_BANKS:
                 nc.vector.tensor_copy(y[:, cols], banks[b][:, : BANK_PIECES[b]])
             else:
@@ -143,7 +147,7 @@ def tile_picked_ranknet_sigmoid_e_kernel(tc, xT, w1_words, w1_scales, offs, win,
 
         y_win = keep.tile([P, V], F32, name="y_win")
         gap = keep.tile([P, V], F32, name="gap")
-        prob = keep.tile([P, V], F32, name="prob")
+        prob = keep.tile([P, V], F32, name="prob", align_bytes=256)
         for i, cols in enumerate(spans(WIN_PIECES)):
             winners = y[:].indirect(win_sb[:, list_cols(cols)])
             if i in VECTOR_WINS:

@@ -20,14 +20,11 @@ PACK = 4
 LIST_ROWS = 16
 BANK = 512
 HALF = S // 2
-GATHER_PIECES = (128, 128, 128, 128)
-VECTOR_WEAVES = 256
-SCALAR_WEAVES = (128, 128)
 PIECE = 128
-SCORE_ORDER = (0, 1, 2, 4, 5, 3, 6, 7)
+VECTOR_ENTRIES = slice(384, 704)
+SCALAR_PIECES = ((128, 256), (192, 128))
 BANK_PIECES = (256, 256, 256, 128, 128)
-BANK_ORDER = (0, 2, 1, 3, 4)
-VECTOR_BANKS = (1, 4)
+VECTOR_BANKS = (2, 4)
 WIN_PIECES = (64, 192, 256)
 VECTOR_WINS = (1,)
 GAP_PIECES = (64, 192, 128)
@@ -86,41 +83,38 @@ def tile_picked_ranknet_sigmoid_e_kernel(tc, xT, w1_words, w1_scales, offs, win,
 
         y = keep.tile([P, S], F32, name="y")
         picked = keep.tile([P, S, PACK], BF16, name="picked", align_bytes=64)
-        first, second = slice(0, HALF), slice(HALF, S)
+        mine = VECTOR_ENTRIES
+        theirs = [slice(0, mine.start), slice(mine.stop, S)]
 
         def offsets(entries):
             return offs_sb[:, list_cols(entries)]
 
-        def words(entries, dtype):
-            return as_words(picked[:, entries, :], dtype).rearrange("p (n u) -> p n u", u=2)
+        def low_words(entries, dtype):
+            return as_words(picked[:, entries, :], dtype).rearrange("p (n u) -> p n u", u=2)[:, :, 0]
 
-        low = keep.tile([P, HALF, 2], BF16, name="low")
-        pairs = keep.tile([P, 2, HALF, 2], BF16, name="pairs")
+        low = keep.tile([P, S, 2], BF16, name="low")
+        for half in spans((HALF, HALF)):
+            for j in (0, 1):
+                nc.vector.tensor_copy(low[:, half, j], rows01[:, j, :].indirect(offsets(half)))
+        for entries in theirs:
+            nc.scalar.copy(low_words(entries, U32), as_words(low[:, entries, :], U32))
+            nc.scalar.activation(picked[:, entries, 2], row2[:].indirect(offsets(entries)), ACT.Copy)
+        nc.vector.tensor_copy(low_words(mine, I32), as_words(low[:, mine, :], I32))
+        dense2 = keep.tile([P, mine.stop - mine.start], BF16, name="dense2")
+        dense3 = keep.tile([P, mine.stop - mine.start], BF16, name="dense3")
+        nc.vector.tensor_copy(dense2[:], row2[:].indirect(offsets(mine)))
+        nc.vector.tensor_copy(picked[:, mine, 2], dense2[:])
 
-        def weave(copy, dtype, entries):
-            held = slice(entries.start - HALF, entries.stop - HALF)
-            copy(words(entries, dtype), pairs[:].rearrange("p u n e -> p u (n e)").bitcast(dtype)[:, :, held].rearrange("p u n -> p n u"))
-
-        for j in (0, 1):
-            nc.vector.tensor_copy(low[:, :, j], rows01[:, j, :].indirect(offsets(first)))
-        nc.scalar.copy(words(first, U32)[:, :, 0], as_words(low[:], U32))
-        for j in (0, 1):
-            nc.vector.tensor_copy(pairs[:, 0, :, j], rows01[:, j, :].indirect(offsets(second)))
-        nc.vector.tensor_copy(pairs[:, 1, :, 0], row2[:].indirect(offsets(second)))
-        nc.scalar.activation(picked[:, first, 2], row2[:].indirect(offsets(first)), ACT.Copy)
-
-        nc.vector.tensor_copy(pairs[:, 1, :, 1], row3[:].indirect(offsets(second)))
-        for entries in spans(GATHER_PIECES):
-            nc.scalar.activation(picked[:, entries, 3], row3[:].indirect(offsets(entries)), ACT.Copy)
-        for entries in spans(SCALAR_WEAVES, HALF + VECTOR_WEAVES):
-            weave(nc.scalar.copy, U32, entries)
+        nc.vector.tensor_copy(dense3[:], row3[:].indirect(offsets(mine)))
+        for part, widths in zip(theirs, SCALAR_PIECES):
+            for entries in spans(widths, part.start):
+                nc.scalar.activation(picked[:, entries, 3], row3[:].indirect(offsets(entries)), ACT.Copy)
 
         bank_cols = spans(BANK_PIECES)
         banks = [psum.tile([P, BANK], F32, name="bank%d" % b) for b in range(len(bank_cols))]
-        for i in SCORE_ORDER:
-            cols = slice(i * PIECE, (i + 1) * PIECE)
+        for i, cols in enumerate(spans((PIECE,) * (S // PIECE))):
             if i == 1:
-                weave(nc.vector.tensor_copy, I32, slice(HALF, HALF + VECTOR_WEAVES))
+                nc.vector.tensor_copy(picked[:, mine, 3], dense3[:])
             codes = keep.tile([P, PIECE], U32, name="codes%d" % i, align_bytes=64)
             scales = keep.tile([P, PIECE], U8, name="scales%d" % i, align_bytes=64)
             nc.vector.quantize_mx(
@@ -138,8 +132,7 @@ def tile_picked_ranknet_sigmoid_e_kernel(tc, xT, w1_words, w1_scales, offs, win,
                 start=True,
                 stop=True,
             )
-        for b in BANK_ORDER:
-            cols = bank_cols[b]
+        for b, cols in enumerate(bank_cols):
             if b in VECTOR_BANKS:
                 nc.vector.tensor_copy(y[:, cols], banks[b][:, : BANK_PIECES[b]])
             else:

@@ -24,7 +24,7 @@ PIECE = 128
 VECTOR_ENTRIES = slice(384, 704)
 SCALAR_PIECES = ((128, 256), (192, 128))
 BANK_PIECES = (256, 256, 256, 128, 128)
-VECTOR_BANKS = (2, 4)
+VECTOR_BANKS = (2, 3)
 WIN_PIECES = (64, 192, 256)
 VECTOR_WINS = (1,)
 GAP_PIECES = (64, 192, 128)

@@ -57,12 +57,14 @@ def tile_picked_ranknet_sigmoid_e_kernel(tc, xT, w1_words, w1_scales, offs, win,
         lose_sb = keep.tile([P, V // LIST_ROWS], U16, name="lose_sb")
         w_codes = keep.tile([P, N], U32, name="w_codes", align_bytes=64)
         w_scale = keep.tile([P, N], U8, name="w_scale", align_bytes=64)
-        rows01 = keep.tile([P, 2, T], F32, name="rows01", align_bytes=256)
+        row0 = keep.tile([P, T], F32, name="row0", align_bytes=256)
+        row1 = keep.tile([P, T], F32, name="row1", align_bytes=256)
         row2 = keep.tile([P, T], F32, name="row2", align_bytes=256)
         row3 = keep.tile([P, T], F32, name="row3", align_bytes=256)
         x_rows = xT.rearrange("(p j) t -> p j t", j=PACK)
 
-        nc.sync.dma_start(out=rows01[:], in_=x_rows[:, 0:2, :])
+        nc.sync.dma_start(out=row0[:], in_=x_rows[:, 0, :])
+        nc.scalar.dma_start(out=row1[:], in_=x_rows[:, 1, :])
         nc.sync.dma_start(offs_sb[:], offs)
         nc.sync.dma_start(out=row2[:], in_=x_rows[:, 2, :])
         nc.sync.dma_start(out=row3[:], in_=x_rows[:, 3, :])
@@ -94,8 +96,8 @@ def tile_picked_ranknet_sigmoid_e_kernel(tc, xT, w1_words, w1_scales, offs, win,
 
         low = keep.tile([P, S, 2], BF16, name="low")
         for half in spans((HALF, HALF)):
-            for j in (0, 1):
-                nc.vector.tensor_copy(low[:, half, j], rows01[:, j, :].indirect(offsets(half)))
+            for j, row in enumerate((row0, row1)):
+                nc.vector.tensor_copy(low[:, half, j], row[:].indirect(offsets(half)))
         for entries in theirs:
             nc.scalar.copy(low_words(entries, U32), as_words(low[:, entries, :], U32))
             nc.scalar.activation(picked[:, entries, 2], row2[:].indirect(offsets(entries)), ACT.Copy)

@@ -20,6 +20,8 @@ PACK = 4
 LIST_ROWS = 16
 BANK = 512
 HALF = S // 2
+QUARTER = S // 4
+ON_SCALAR_QUEUE = 6208
 PIECE = 128
 VECTOR_ENTRIES = slice(384, 704)
 SCALAR_PIECES = ((128, 256), (192, 128))
@@ -57,17 +59,16 @@ def tile_picked_ranknet_sigmoid_e_kernel(tc, xT, w1_words, w1_scales, offs, win,
         lose_sb = keep.tile([P, V // LIST_ROWS], U16, name="lose_sb")
         w_codes = keep.tile([P, N], U32, name="w_codes", align_bytes=64)
         w_scale = keep.tile([P, N], U8, name="w_scale", align_bytes=64)
-        row0 = keep.tile([P, T], F32, name="row0", align_bytes=256)
-        row1 = keep.tile([P, T], F32, name="row1", align_bytes=256)
+        rows01 = keep.tile([P, 2 * T], F32, name="rows01", align_bytes=256)
         row2 = keep.tile([P, T], F32, name="row2", align_bytes=256)
         row3 = keep.tile([P, T], F32, name="row3", align_bytes=256)
-        x_rows = xT.rearrange("(p j) t -> p j t", j=PACK)
+        x_rows = xT.rearrange("(p j) t -> p (j t)", j=PACK)
 
-        nc.sync.dma_start(out=row0[:], in_=x_rows[:, 0, :])
-        nc.scalar.dma_start(out=row1[:], in_=x_rows[:, 1, :])
+        nc.sync.dma_start(out=row2[:], in_=x_rows[:, 2 * T : 3 * T])
+        nc.scalar.dma_start(out=rows01[:, :ON_SCALAR_QUEUE], in_=x_rows[:, :ON_SCALAR_QUEUE])
         nc.sync.dma_start(offs_sb[:], offs)
-        nc.sync.dma_start(out=row2[:], in_=x_rows[:, 2, :])
-        nc.sync.dma_start(out=row3[:], in_=x_rows[:, 3, :])
+        nc.sync.dma_start(out=rows01[:, ON_SCALAR_QUEUE:], in_=x_rows[:, ON_SCALAR_QUEUE : 2 * T])
+        nc.sync.dma_start(out=row3[:], in_=x_rows[:, 3 * T :])
         nc.sync.dma_start(out=w_codes[:].bitcast(I32), in_=w1_words[0].rearrange("p n t -> p (n t)").bitcast(I32))
         nc.vector.memset(w_scale[:].bitcast(I32), 0)
         for q in range(4):
@@ -94,18 +95,26 @@ def tile_picked_ranknet_sigmoid_e_kernel(tc, xT, w1_words, w1_scales, offs, win,
         def low_words(entries, dtype):
             return as_words(picked[:, entries, :], dtype).rearrange("p (n u) -> p n u", u=2)[:, :, 0]
 
-        low = keep.tile([P, S, 2], BF16, name="low")
-        for half in spans((HALF, HALF)):
-            for j, row in enumerate((row0, row1)):
-                nc.vector.tensor_copy(low[:, half, j], row[:].indirect(offsets(half)))
-        for entries in theirs:
-            nc.scalar.copy(low_words(entries, U32), as_words(low[:, entries, :], U32))
-            nc.scalar.activation(picked[:, entries, 2], row2[:].indirect(offsets(entries)), ACT.Copy)
-        nc.vector.tensor_copy(low_words(mine, I32), as_words(low[:, mine, :], I32))
         dense2 = keep.tile([P, mine.stop - mine.start], BF16, name="dense2")
         dense3 = keep.tile([P, mine.stop - mine.start], BF16, name="dense3")
         nc.vector.tensor_copy(dense2[:], row2[:].indirect(offsets(mine)))
         nc.vector.tensor_copy(picked[:, mine, 2], dense2[:])
+        for entries in theirs:
+            nc.scalar.activation(picked[:, entries, 2], row2[:].indirect(offsets(entries)), ACT.Copy)
+
+        head, paired, rear = spans((QUARTER, HALF, QUARTER))
+        low = keep.tile([P, HALF, 2], BF16, name="low")
+        low_head = keep.tile([P, 2, QUARTER], F32, name="low_head")
+        low_rear = keep.tile([P, 2, QUARTER], F32, name="low_rear")
+        windows = [rows01[:, j * T : (j + 1) * T] for j in (0, 1)]
+        for entries, held in ((head, low_head), (rear, low_rear)):
+            for j in (0, 1):
+                nc.scalar.activation(held[:, j, :], windows[j].indirect(offsets(entries)), ACT.Copy)
+        for j in (0, 1):
+            nc.vector.tensor_copy(low[:, :, j], windows[j].indirect(offsets(paired)))
+        nc.vector.tensor_copy(picked[:, head, 0:2], low_head[:].rearrange("p j n -> p n j"))
+        nc.vector.tensor_copy(low_words(paired, I32), as_words(low[:], I32))
+        nc.scalar.copy(picked[:, rear, 0:2], low_rear[:].rearrange("p j n -> p n j"))
 
         nc.vector.tensor_copy(dense3[:], row3[:].indirect(offsets(mine)))
         for part, widths in zip(theirs, SCALAR_PIECES):

@@ -114,7 +114,9 @@ def tile_picked_ranknet_sigmoid_e_kernel(tc, xT, w1_words, w1_scales, offs, win,
             nc.vector.tensor_copy(low[:, :, j], windows[j].indirect(offsets(paired)))
         nc.vector.tensor_copy(picked[:, head, 0:2], low_head[:].rearrange("p j n -> p n j"))
         nc.vector.tensor_copy(low_words(paired, I32), as_words(low[:], I32))
-        nc.scalar.copy(picked[:, rear, 0:2], low_rear[:].rearrange("p j n -> p n j"))
+        for copy, part in zip((nc.vector.tensor_copy, nc.scalar.copy), spans((PIECE, PIECE))):
+            entries = slice(rear.start + part.start, rear.start + part.stop)
+            copy(picked[:, entries, 0:2], low_rear[:, :, part].rearrange("p j n -> p n j"))
 
         nc.vector.tensor_copy(dense3[:], row3[:].indirect(offsets(mine)))
         for part, widths in zip(theirs, SCALAR_PIECES):

@@ -32,7 +32,7 @@ VECTOR_WINS = (1,)
 GAP_PIECES = (64, 192, 128)
 SCALAR_LOSERS = 128
 SIGMOID_PIECES = (64, 192, 128, 128)
-STORE_PIECES = (64, 192, 256)
+STORE_PIECES = (64, 192, 128, 128)
 
 
 def spans(widths, first=0):
@@ -168,5 +168,7 @@ def tile_picked_ranknet_sigmoid_e_kernel(tc, xT, w1_words, w1_scales, offs, win,
         nc.vector.tensor_tensor(gap[:, tail], y_lose[:], y_win[:, tail], ALU.subtract)
         for cols in spans(SIGMOID_PIECES):
             nc.scalar.activation(prob[:, cols], gap[:, cols], ACT.Sigmoid, scale=-1.0)
-        for cols in spans(STORE_PIECES):
+        stores = spans(STORE_PIECES)
+        for cols in stores[:-1]:
             nc.sync.dma_start(out=out[:, cols], in_=prob[:, cols])
+        nc.scalar.dma_start(out=out[:, stores[-1]], in_=prob[:, stores[-1]])

@@ -23,10 +23,11 @@ HALF = S // 2
 QUARTER = S // 4
 ON_SCALAR_QUEUE = 6208
 PIECE = 128
-VECTOR_ENTRIES = slice(384, 704)
-SCALAR_PIECES = ((128, 256), (192, 128))
-BANK_PIECES = (256, 256, 256, 128, 128)
-VECTOR_BANKS = (2, 3)
+VECTOR_ENTRIES = slice(384, 736)
+SCALAR_PIECES = ((128, 256), (160, 128))
+PASSES = (128,) * 7 + (64, 64)
+BANK_PIECES = (256, 256, 128, 128, 128, 64, 64)
+VECTOR_BANKS = (1, 3, 5)
 WIN_PIECES = (64, 192, 256)
 VECTOR_WINS = (1,)
 GAP_PIECES = (64, 192, 128)
@@ -125,11 +126,12 @@ def tile_picked_ranknet_sigmoid_e_kernel(tc, xT, w1_words, w1_scales, offs, win,
 
         bank_cols = spans(BANK_PIECES)
         banks = [psum.tile([P, BANK], F32, name="bank%d" % b) for b in range(len(bank_cols))]
-        for i, cols in enumerate(spans((PIECE,) * (S // PIECE))):
+        for i, cols in enumerate(spans(PASSES)):
+            width = cols.stop - cols.start
             if i == 1:
                 nc.vector.tensor_copy(picked[:, mine, 3], dense3[:])
-            codes = keep.tile([P, PIECE], U32, name="codes%d" % i, align_bytes=64)
-            scales = keep.tile([P, PIECE], U8, name="scales%d" % i, align_bytes=64)
+            codes = keep.tile([P, width], U32, name="codes%d" % i, align_bytes=64)
+            scales = keep.tile([P, width], U8, name="scales%d" % i, align_bytes=64)
             nc.vector.quantize_mx(
                 out=codes[:].bitcast(FP8X4),
                 scales=scales[:],

from contextlib import ExitStack

import concourse.mybir as mybir

K, T, S, V, N = 512, 4096, 1024, 512, 128
FLOPS = 2 * K * S * N

F32 = mybir.dt.float32
BF16 = mybir.dt.bfloat16
I32 = mybir.dt.int32
U32 = mybir.dt.uint32
U16 = mybir.dt.uint16
U8 = mybir.dt.uint8
FP8X4 = mybir.dt.float8_e4m3fn_x4
ACT = mybir.ActivationFunctionType
ALU = mybir.AluOpType

P = 128
PACK = 4
LIST_ROWS = 16
BANK = 512
HALF = S // 2
QUARTER = S // 4
ON_SCALAR_QUEUE = 6208
PIECE = 128
VECTOR_ENTRIES = slice(384, 736)
SCALAR_PIECES = ((128, 256), (160, 128))
PASSES = (128,) * 7 + (64, 64)
BANK_PIECES = (256, 256, 128, 128, 128, 64, 64)
VECTOR_BANKS = (1, 3, 5)
WIN_PIECES = (64, 192, 256)
VECTOR_WINS = (1,)
GAP_PIECES = (64, 192, 128)
SCALAR_LOSERS = 128
SIGMOID_PIECES = (64, 192, 128, 128)
STORE_PIECES = (64, 192, 128, 128)


def spans(widths, first=0):
    starts = [first + sum(widths[:i]) for i in range(len(widths))]
    return [slice(a, a + w) for a, w in zip(starts, widths)]


def list_cols(entries):
    return slice(entries.start // LIST_ROWS, entries.stop // LIST_ROWS)


def as_words(pairs, dtype):
    return pairs.rearrange("p n e -> p (n e)").bitcast(dtype)


def tile_picked_ranknet_sigmoid_e_kernel(tc, xT, w1_words, w1_scales, offs, win, lose, out):
    nc = tc.nc
    with ExitStack() as ctx:
        keep = ctx.enter_context(tc.tile_pool(name="keep", bufs=1))
        psum = ctx.enter_context(tc.psum_pool(name="psum", bufs=1))

        offs_sb = keep.tile([P, S // LIST_ROWS], U16, name="offs_sb")
        win_sb = keep.tile([P, V // LIST_ROWS], U16, name="win_sb")
        lose_sb = keep.tile([P, V // LIST_ROWS], U16, name="lose_sb")
        w_codes = keep.tile([P, N], U32, name="w_codes", align_bytes=64)
        w_scale = keep.tile([P, N], U8, name="w_scale", align_bytes=64)
        rows01 = keep.tile([P, 2 * T], F32, name="rows01", align_bytes=256)
        row2 = keep.tile([P, T], F32, name="row2", align_bytes=256)
        row3 = keep.tile([P, T], F32, name="row3", align_bytes=256)
        x_rows = xT.rearrange("(p j) t -> p (j t)", j=PACK)

        nc.sync.dma_start(out=row2[:], in_=x_rows[:, 2 * T : 3 * T])
        nc.scalar.dma_start(out=rows01[:, :ON_SCALAR_QUEUE], in_=x_rows[:, :ON_SCALAR_QUEUE])
        nc.sync.dma_start(offs_sb[:], offs)
        nc.sync.dma_start(out=rows01[:, ON_SCALAR_QUEUE:], in_=x_rows[:, ON_SCALAR_QUEUE : 2 * T])
        nc.sync.dma_start(out=row3[:], in_=x_rows[:, 3 * T :])
        nc.sync.dma_start(out=w_codes[:].bitcast(I32), in_=w1_words[0].rearrange("p n t -> p (n t)").bitcast(I32))
        nc.vector.memset(w_scale[:].bitcast(I32), 0)
        for q in range(4):
            nc.sync.dma_start(
                out=w_scale[:].bitcast(I32)[32 * q : 32 * q + 4, :],
                in_=w1_scales[0, 4 * q : 4 * q + 4, :].bitcast(I32),
            )
        nc.sync.dma_start(win_sb[:], win)
        nc.sync.dma_start(lose_sb[:], lose)

        warm_in = keep.tile([P, 1], F32, name="warm_in")
        warm_out = keep.tile([P, 1], F32, name="warm_out")
        nc.vector.memset(warm_in[:], 0.0)
        nc.scalar.activation(warm_out[:], warm_in[:], ACT.Sigmoid)

        y = keep.tile([P, S], F32, name="y")
        picked = keep.tile([P, S, PACK], BF16, name="picked", align_bytes=64)
        mine = VECTOR_ENTRIES
        theirs = [slice(0, mine.start), slice(mine.stop, S)]

        def offsets(entries):
            return offs_sb[:, list_cols(entries)]

        def low_words(entries, dtype):
            return as_words(picked[:, entries, :], dtype).rearrange("p (n u) -> p n u", u=2)[:, :, 0]

        dense2 = keep.tile([P, mine.stop - mine.start], BF16, name="dense2")
        dense3 = keep.tile([P, mine.stop - mine.start], BF16, name="dense3")
        nc.vector.tensor_copy(dense2[:], row2[:].indirect(offsets(mine)))
        nc.vector.tensor_copy(picked[:, mine, 2], dense2[:])
        for entries in theirs:
            nc.scalar.activation(picked[:, entries, 2], row2[:].indirect(offsets(entries)), ACT.Copy)

        head, paired, rear = spans((QUARTER, HALF, QUARTER))
        low = keep.tile([P, HALF, 2], BF16, name="low")
        low_head = keep.tile([P, 2, QUARTER], F32, name="low_head")
        low_rear = keep.tile([P, 2, QUARTER], F32, name="low_rear")
        windows = [rows01[:, j * T : (j + 1) * T] for j in (0, 1)]
        for entries, held in ((head, low_head), (rear, low_rear)):
            for j in (0, 1):
                nc.scalar.activation(held[:, j, :], windows[j].indirect(offsets(entries)), ACT.Copy)
        for j in (0, 1):
            nc.vector.tensor_copy(low[:, :, j], windows[j].indirect(offsets(paired)))
        nc.vector.tensor_copy(picked[:, head, 0:2], low_head[:].rearrange("p j n -> p n j"))
        nc.vector.tensor_copy(low_words(paired, I32), as_words(low[:], I32))
        for copy, part in zip((nc.vector.tensor_copy, nc.scalar.copy), spans((PIECE, PIECE))):
            entries = slice(rear.start + part.start, rear.start + part.stop)
            copy(picked[:, entries, 0:2], low_rear[:, :, part].rearrange("p j n -> p n j"))

        nc.vector.tensor_copy(dense3[:], row3[:].indirect(offsets(mine)))
        for part, widths in zip(theirs, SCALAR_PIECES):
            for entries in spans(widths, part.start):
                nc.scalar.activation(picked[:, entries, 3], row3[:].indirect(offsets(entries)), ACT.Copy)

        bank_cols = spans(BANK_PIECES)
        banks = [psum.tile([P, BANK], F32, name="bank%d" % b) for b in range(len(bank_cols))]
        for i, cols in enumerate(spans(PASSES)):
            width = cols.stop - cols.start
            if i == 1:
                nc.vector.tensor_copy(picked[:, mine, 3], dense3[:])
            codes = keep.tile([P, width], U32, name="codes%d" % i, align_bytes=64)
            scales = keep.tile([P, width], U8, name="scales%d" % i, align_bytes=64)
            nc.vector.quantize_mx(
                out=codes[:].bitcast(FP8X4),
                scales=scales[:],
                in_=picked[:, cols, :].rearrange("p n j -> p (n j)"),
            )
            b = max(b for b, held in enumerate(bank_cols) if held.start <= cols.start)
            nc.tensor.matmul_mx(
                out=banks[b][:, cols.start - bank_cols[b].start : cols.stop - bank_cols[b].start],
                lhsT=w_codes[:].bitcast(FP8X4),
                lhsT_scale=w_scale[:],
                rhs=codes[:].bitcast(FP8X4),
                rhs_scale=scales[:],
                start=True,
                stop=True,
            )
        for b, cols in enumerate(bank_cols):
            if b in VECTOR_BANKS:
                nc.vector.tensor_copy(y[:, cols], banks[b][:, : BANK_PIECES[b]])
            else:
                nc.scalar.activation(y[:, cols], banks[b][:, : BANK_PIECES[b]], ACT.Copy)

        y_win = keep.tile([P, V], F32, name="y_win")
        gap = keep.tile([P, V], F32, name="gap")
        prob = keep.tile([P, V], F32, name="prob", align_bytes=256)
        for i, cols in enumerate(spans(WIN_PIECES)):
            winners = y[:].indirect(win_sb[:, list_cols(cols)])
            if i in VECTOR_WINS:
                nc.vector.tensor_copy(y_win[:, cols], winners)
            else:
                nc.scalar.activation(y_win[:, cols], winners, ACT.Copy)
        tail = slice(V - SCALAR_LOSERS, V)
        y_lose = keep.tile([P, SCALAR_LOSERS], F32, name="y_lose")
        nc.scalar.activation(y_lose[:], y[:].indirect(lose_sb[:, list_cols(tail)]), ACT.Copy)
        for cols in spans(GAP_PIECES):
            nc.vector.tensor_tensor(gap[:, cols], y[:].indirect(lose_sb[:, list_cols(cols)]), y_win[:, cols], ALU.subtract)
        nc.vector.tensor_tensor(gap[:, tail], y_lose[:], y_win[:, tail], ALU.subtract)
        for cols in spans(SIGMOID_PIECES):
            nc.scalar.activation(prob[:, cols], gap[:, cols], ACT.Sigmoid, scale=-1.0)
        stores = spans(STORE_PIECES)
        for cols in stores[:-1]:
            nc.sync.dma_start(out=out[:, cols], in_=prob[:, cols])
        nc.scalar.dma_start(out=out[:, stores[-1]], in_=prob[:, stores[-1]])
